import numpy as np
import ml_dtypes


def mxq(x, axis, fmt="e4m3"):
    dtype, down = {"e4m3": (ml_dtypes.float8_e4m3fn, 7), "e5m2": (ml_dtypes.float8_e5m2, 14)}[fmt]
    v = np.moveaxis(np.asarray(x, np.float32).astype(ml_dtypes.bfloat16).astype(np.float64), axis, -1)
    blocks = v.reshape(v.shape[:-1] + (-1, 32))
    amax = np.abs(blocks).max(-1, keepdims=True)
    byte = np.maximum(np.where(amax > 0, np.frexp(amax)[1] - 1 + 127, 0) - down, 1)
    scale = np.exp2(byte - 127.0)
    codes = (blocks / scale).astype(np.float32).astype(dtype).astype(np.float64)
    return np.moveaxis((codes * scale).reshape(v.shape), -1, axis)


WIDE = False


def mx_kscale(k):
    if not WIDE:
        return np.ones(k)
    levels = np.array([24, -24, 12, -12, 0])
    if k % 512:
        return np.exp2(np.random.permutation(np.resize(levels, k // 32))).repeat(32)
    a = np.empty((k // 512, 16))
    for p in range(k // 512):
        a[p, :8] = np.random.permutation(np.resize(levels, 8))
        for g in range(8):
            far = levels[np.abs(levels - a[p, g]) >= 10]
            a[p, g + 8] = far[np.random.randint(len(far))]
    return np.exp2(a.ravel()).repeat(32)


def f64(x):
    return np.asarray(x).astype(np.float64)


def striped(idx):
    return np.tile(idx.reshape(-1, 16).T, (8, 1)).astype(np.uint16)


def unstriped(offs):
    return offs[:16].T.reshape(-1).astype(np.int64)


E2M1 = np.array([0.0, 0.5, 1.0, 1.5, 2.0, 3.0, 4.0, 6.0, -0.0, -0.5, -1.0, -1.5, -2.0, -3.0, -4.0, -6.0])


def pack_weight(w, fmt):
    k, n = w.shape
    w = f64(np.asarray(w, np.float32).astype(ml_dtypes.bfloat16)).reshape(k // 32, 32, n)
    amax = np.abs(w).max(1)
    if fmt == "e4m3":
        byte = np.frexp(amax)[1] - 1 + 127 - 7
    else:
        mant, ex = np.frexp(amax / 6.0)
        byte = np.where(mant > 0.5, ex, ex - 1) + 127
    byte = np.clip(np.where(amax > 0, byte, 1), 1, 254)
    scaled = (w * np.exp2(127.0 - byte)[:, None, :]).reshape(k, n).astype(np.float32)
    by_word = np.ascontiguousarray(scaled.reshape(k // 512, 128, 4, n).transpose(0, 1, 3, 2))
    if fmt == "e4m3":
        words = by_word.astype(ml_dtypes.float8_e4m3fn).view(np.uint8)
    else:
        c = by_word.astype(ml_dtypes.float4_e2m1fn).view(np.uint8) & 0xF
        words = (c[..., 0::2] | (c[..., 1::2] << 4)).reshape(k // 512, 128, 2 * n)
    return np.ascontiguousarray(words), np.ascontiguousarray(byte.astype(np.uint8).reshape(k // 512, 16, n))


def unpack_weight(words, scales, fmt):
    g, _, n = scales.shape
    words = np.ascontiguousarray(words).reshape(g, 128, n, -1)
    if fmt == "e4m3":
        vals = words.view(ml_dtypes.float8_e4m3fn).astype(np.float64)
    else:
        nib = np.empty((g, 128, n, 4), np.uint8)
        nib[..., 0::2] = words & 0xF
        nib[..., 1::2] = words >> 4
        vals = E2M1[nib]
    vals = vals * np.repeat(np.exp2(scales.astype(np.float64) - 127.0), 8, axis=1)[..., None]
    return vals.transpose(0, 1, 3, 2).reshape(g * 512, n)


def pack_table4(v):
    words, scales = pack_weight(v, "e2m1")
    g, t = words.shape[0] // 2, v.shape[1]
    return np.ascontiguousarray(words.reshape(g, 2, 128, t, 2).transpose(0, 2, 3, 1, 4).reshape(g, 128, t, 4)), scales


def unpack_table4(words, scales):
    g, _, t, _ = words.shape
    return unpack_weight(words.reshape(g, 128, t, 2, 2).transpose(0, 3, 1, 2, 4).reshape(2 * g, 128, 2 * t), scales, "e2m1")


K, F, N, T, J = 1024, 1024, 256, 4096, 1024


def setup_inputs():
    n = np.random.standard_normal
    s = mx_kscale(K)[:, None]
    u = mx_kscale(F)[:, None]
    p_tab = pack_table4(n((K, T)) * s)
    return {
        "tab_words": p_tab[0],
        "tab_scales": p_tab[1],
        "co": (n((K, F)) / np.sqrt(K) / s).astype(np.float32),
        "si": (n((K, F)) / np.sqrt(K) / s).astype(np.float32),
        "gn": (np.random.uniform(0.5, 2.0, F) * u[:, 0]).astype(np.float32),
        "fb": (np.abs(n((F, N))) / F / u).astype(np.float32),
        "offs": striped(np.random.permutation(T)[:J]),
    }


def reference(tab_words, tab_scales, co, si, gn, fb, offs):
    idx = unstriped(offs)
    tab_ = unpack_table4(tab_words, tab_scales)[:, idx]
    co_ = mxq(f64(co), 0, "e4m3")
    si_ = mxq(f64(si), 0, "e4m3")
    re = co_.T @ tab_
    im = si_.T @ tab_
    h = f64(gn)[:, None] * ((re) ** 2 + (im) ** 2)
    h_ = mxq(h, 0, "e4m3")
    fb_ = mxq(f64(fb), 0, "e4m3")
    y = fb_.T @ h_
    return y

@@ -1,0 +1,269 @@
+from contextlib import ExitStack
+
+import concourse.mybir as mybir
+
+K, F, N, T, J = 1024, 1024, 256, 4096, 1024
+FLOPS = 2 * (2 * K * F * J + F * N * J)
+
+F32 = mybir.dt.float32
+BF16 = mybir.dt.bfloat16
+I32 = mybir.dt.int32
+U32 = mybir.dt.uint32
+U16 = mybir.dt.uint16
+U8 = mybir.dt.uint8
+FP8X4 = mybir.dt.float8_e4m3fn_x4
+FP4X4 = mybir.dt.float4_e2m1fn_x4
+ALU = mybir.AluOpType
+ACT = mybir.ActivationFunctionType
+
+P = 128
+PACK = 4
+PASS = P * PACK
+BANK = 512
+TINY = 2.0 ** -70
+
+
+def tile_list_meltab_pow_kernel(tc, tab_words, tab_scales, co, si, gn, fb, offs, out):
+    nc = tc.nc
+    with ExitStack() as ctx:
+        keep = ctx.enter_context(tc.tile_pool(name="keep", bufs=1))
+        raws = ctx.enter_context(tc.tile_pool(name="raws", bufs=4))
+        casts = ctx.enter_context(tc.tile_pool(name="casts", bufs=4))
+        squares = ctx.enter_context(tc.tile_pool(name="squares", bufs=3))
+        powers = ctx.enter_context(tc.tile_pool(name="powers", bufs=3))
+        results = ctx.enter_context(tc.tile_pool(name="results", bufs=3))
+        psum = ctx.enter_context(tc.psum_pool(name="psum", bufs=8))
+
+        offsets = keep.tile([P, J // 16], U16, name="offsets")
+        nc.sync.dma_start(offsets[:], offs)
+
+        scale_store = keep.tile([P, T // 4], I32, name="w_codes_re00", align_bytes=64)
+        nc.gpsimd.memset(scale_store[:], 0)
+        scale_rows = tab_scales.bitcast(I32)
+
+        def load_scales():
+            for q in range(4):
+                nc.sync.dma_start(out=scale_store[32 * q : 32 * q + 8, :], in_=scale_rows[:, 4 * q : 4 * q + 4, :])
+
+        gain = keep.tile([P, 2, PACK], F32, name="gain")
+        nc.sync.dma_start(out=gain[:], in_=gn.rearrange("(g p t) -> p g t", g=2, t=PACK))
+
+        weights = {"re": co, "im": si}
+        raw, grouped, w_codes, w_scales, squared = {}, {}, {}, {}, {}
+
+        def load(part, a, g):
+            tile = raws.tile([P, PACK, BANK], F32, name="raw", align_bytes=64)
+            rows = weights[part][a * PASS : (a + 1) * PASS, g * BANK : (g + 1) * BANK]
+            nc.sync.dma_start(out=tile[:], in_=rows.rearrange("(p i) f -> p i f", i=PACK))
+            raw[part, a, g] = tile
+
+        def cast(part, a, g, engine):
+            tile = casts.tile([P, PACK * BANK], BF16, name="grouped", align_bytes=64)
+            dst = tile[:].rearrange("p (t m i) -> p m i t", t=PACK, i=PACK)
+            src = raw[part, a, g][:].rearrange("p i (m t) -> p m i t", t=PACK)
+            if engine == "scalar":
+                nc.scalar.copy(out=dst, in_=src)
+            elif engine == "split":
+                nc.vector.tensor_copy(out=dst[:, : P // 2], in_=src[:, : P // 2])
+                nc.scalar.copy(out=dst[:, P // 2 :], in_=src[:, P // 2 :])
+            else:
+                nc.vector.tensor_copy(out=dst, in_=src)
+            grouped[part, a, g] = tile
+
+        def quantise_weight(part, a, g):
+            codes = keep.tile([P, BANK], U32, name="w_codes_%s%d%d" % (part, a, g), align_bytes=64)
+            scales = keep.tile([P, BANK], U8, name="w_scales_%s%d%d" % (part, a, g), align_bytes=64)
+            nc.vector.quantize_mx(out=codes[:].bitcast(FP8X4), scales=scales[:], in_=grouped[part, a, g][:])
+            w_codes[part, a, g], w_scales[part, a, g] = codes, scales
+
+        word_store = keep.tile([P, T], I32, name="word_store", align_bytes=64)
+        picked_scales = [keep.tile([P, J], U8, name="picked_scales%d" % a, align_bytes=64) for a in range(2)]
+        picked_words = {}
+        frames = [keep.tile([P, 2, 2 * BANK], U8, name="frames%d" % h, align_bytes=64) for h in range(2)]
+
+        def load_table():
+            nc.sync.dma_start(out=word_store[:], in_=tab_words[0].rearrange("p t b -> p (t b)").bitcast(I32))
+
+        def gather_scales():
+            window = scale_store[:].bitcast(U8)
+            nc.vector.tensor_copy(picked_scales[0][:], window.indirect(offsets[:]))
+            nc.gpsimd.memset(picked_scales[1][:].bitcast(I32), 0)
+            nc.scalar.dma_start(out=picked_scales[1][0:112, :].bitcast(I32), in_=picked_scales[0][4:116, :].bitcast(I32))
+
+        def gather_words(h):
+            picked_words[h] = keep.tile([P, BANK], U32, name="picked_words", align_bytes=64)
+            window = word_store[:].bitcast(U32)
+            nc.vector.tensor_copy(picked_words[h][:], window.indirect(offsets[:, 32 * h : 32 * (h + 1)]))
+
+        def part_words(h):
+            nc.vector.tensor_copy(
+                out=frames[h][:].bitcast(U16),
+                in_=picked_words[h][:].bitcast(U16).rearrange("p (j a) -> p a j", a=2),
+            )
+
+        root = keep.tile([P, 2 * PACK], F32, name="root")
+        sign = keep.tile([P, 2, PACK], F32, name="sign")
+
+        def prepare_gain():
+            flat = gain[:].rearrange("p g t -> p (g t)")
+            size = keep.tile([P, 2 * PACK], F32, name="size")
+            guess = keep.tile([P, 2 * PACK], F32, name="guess")
+            safe = keep.tile([P, 2 * PACK], F32, name="safe")
+            inverse = keep.tile([P, 2 * PACK], F32, name="inverse")
+            ratio = keep.tile([P, 2 * PACK], F32, name="ratio")
+            total = keep.tile([P, 2 * PACK], F32, name="total")
+            twice = keep.tile([P, 2 * PACK], F32, name="twice")
+            nc.vector.scalar_tensor_tensor(out=size[:], in0=flat, scalar=-1.0, in1=flat, op0=ALU.mult, op1=ALU.max)
+            nc.scalar.activation(out=guess[:], in_=size[:], func=ACT.Sqrt)
+            nc.vector.tensor_scalar(out=twice[:], in0=flat, scalar1=0.0, scalar2=2.0, op0=ALU.is_ge, op1=ALU.mult)
+            nc.vector.tensor_scalar(out=sign[:].rearrange("p g t -> p (g t)"), in0=twice[:], scalar1=-1.0, scalar2=None, op0=ALU.add)
+            nc.vector.tensor_scalar(out=safe[:], in0=guess[:], scalar1=TINY, scalar2=None, op0=ALU.max)
+            nc.vector.reciprocal(out=inverse[:], in_=safe[:])
+            nc.vector.tensor_tensor(out=ratio[:], in0=size[:], in1=inverse[:], op=ALU.mult)
+            nc.vector.tensor_tensor(out=total[:], in0=ratio[:], in1=guess[:], op=ALU.add)
+            nc.vector.tensor_scalar(out=root[:], in0=total[:], scalar1=0.5, scalar2=None, op0=ALU.mult)
+
+        def transform(part, g, h, pieces=1):
+            tile = squares.tile([P, PACK, BANK], F32, name="squared_" + part, align_bytes=64)
+            banks = []
+            for t in range(PACK):
+                bank = psum.tile([P, BANK], F32, name="bank")
+                cols = slice(t * P, (t + 1) * P)
+                for a in range(2):
+                    nc.tensor.matmul_mx(
+                        out=bank[:],
+                        lhsT=w_codes[part, a, g][:, cols].bitcast(FP8X4),
+                        lhsT_scale=w_scales[part, a, g][:, cols],
+                        rhs=frames[h][:, a, :].bitcast(FP4X4),
+                        rhs_scale=picked_scales[a][:, h * BANK : (h + 1) * BANK],
+                        start=(a == 0),
+                        stop=(a == 1),
+                    )
+                banks.append(bank)
+            width = BANK // pieces
+            for c in range(pieces):
+                cols = slice(c * width, (c + 1) * width)
+                for t in range(PACK):
+                    column = PACK * g + t
+                    nc.scalar.activation(out=tile[:, t, cols], in_=banks[t][:, cols], func=ACT.Square, scale=root[:, column : column + 1])
+            squared[part, g, h] = tile
+
+        h_codes = [keep.tile([P, J], U32, name="h_codes%d" % g, align_bytes=64) for g in range(2)]
+        h_scales = [keep.tile([P, J], U8, name="h_scales%d" % g, align_bytes=64) for g in range(2)]
+        power = {}
+
+        def add_squares(g, h, lo, width):
+            tile = powers.tile([P, PACK * BANK], BF16, name="power", align_bytes=64)
+            cols = slice(lo, lo + width)
+            nc.vector.tensor_tensor(
+                out=tile[:, : PACK * width].rearrange("p (c i t) -> p c t i", i=4, t=PACK),
+                in0=squared["re", g, h][:, :, cols].rearrange("p t (c i) -> p c t i", i=4),
+                in1=squared["im", g, h][:, :, cols].rearrange("p t (c i) -> p c t i", i=4),
+                op=ALU.add,
+            )
+            power[g, h, lo] = tile
+
+        def quantise_power(g, h, lo, width):
+            cols = slice(h * BANK + lo, h * BANK + lo + width)
+            nc.vector.quantize_mx(out=h_codes[g][:, cols].bitcast(FP8X4), scales=h_scales[g][:, cols], in_=power[g, h, lo][:, : PACK * width])
+
+        fb_codes = keep.tile([P, 2 * N], U32, name="fb_codes", align_bytes=64)
+        fb_scales = keep.tile([P, 2 * N], U8, name="fb_scales", align_bytes=64)
+
+        def load_filters():
+            tile = raws.tile([P, 2, PACK, N], F32, name="raw", align_bytes=64)
+            nc.sync.dma_start(out=tile[:], in_=fb.rearrange("(g p t) n -> p g t n", g=2, t=PACK))
+            raw["fb"] = tile
+
+        def cast_filters():
+            tile = casts.tile([P, 2, PACK * N], BF16, name="grouped", align_bytes=64)
+            for g in range(2):
+                nc.vector.tensor_tensor(
+                    out=tile[:, g, :].rearrange("p (c i t) -> p c t i", i=4, t=PACK),
+                    in0=raw["fb"][:, g, :, :].rearrange("p t (c i) -> p c t i", i=4),
+                    in1=sign[:, g, :].unsqueeze(1).unsqueeze(3).to_broadcast([P, N // 4, PACK, 4]),
+                    op=ALU.mult,
+                )
+            grouped["fb"] = tile
+
+        def quantise_filters():
+            nc.vector.quantize_mx(out=fb_codes[:].bitcast(FP8X4), scales=fb_scales[:], in_=grouped["fb"][:].rearrange("p g w -> p (g w)"))
+
+        def filter_bank(lo, width, engine):
+            frames_cols = slice(lo, lo + width)
+            result = results.tile([P, 2, BANK], F32, name="result", align_bytes=64)
+            for b in range(2):
+                bank = psum.tile([P, BANK], F32, name="bank")
+                for g in range(2):
+                    cols = slice(g * N + b * P, g * N + (b + 1) * P)
+                    nc.tensor.matmul_mx(
+                        out=bank[:, :width],
+                        lhsT=fb_codes[:, cols].bitcast(FP8X4),
+                        lhsT_scale=fb_scales[:, cols],
+                        rhs=h_codes[g][:, frames_cols].bitcast(FP8X4),
+                        rhs_scale=h_scales[g][:, frames_cols],
+                        start=(g == 0),
+                        stop=(g == 1),
+                    )
+                if engine == "scalar" or (engine == "both" and b == 0):
+                    nc.scalar.copy(out=result[:, b, :width], in_=bank[:, :width])
+                else:
+                    nc.vector.tensor_copy(out=result[:, b, :width], in_=bank[:, :width])
+            nc.sync.dma_start(out=out.rearrange("(b p) j -> p b j", p=P)[:, :, frames_cols], in_=result[:, :, :width])
+
+        load_scales()
+        load("re", 0, 0)
+        load_table()
+        load("re", 1, 0)
+        gather_scales()
+        gather_words(0)
+        load("im", 1, 0)
+        load("im", 0, 0)
+        cast("im", 1, 0, "vector")
+        cast("im", 0, 0, "vector")
+        part_words(0)
+        cast("re", 0, 0, "split")
+        cast("re", 1, 0, "split")
+        load("re", 0, 1)
+        load("re", 1, 1)
+        cast("re", 1, 1, "vector")
+        quantise_weight("im", 1, 0)
+        prepare_gain()
+        quantise_weight("im", 0, 0)
+        cast("re", 0, 1, "vector")
+        quantise_weight("re", 1, 1)
+        quantise_weight("re", 0, 0)
+        quantise_weight("re", 1, 0)
+        load("im", 0, 1)
+        cast("im", 0, 1, "scalar")
+        load("im", 1, 1)
+        gather_words(1)
+        transform("im", 0, 0)
+        part_words(1)
+        cast("im", 1, 1, "split")
+        quantise_weight("re", 0, 1)
+        transform("im", 0, 1)
+        quantise_weight("im", 1, 1)
+        quantise_weight("im", 0, 1)
+        transform("re", 1, 0)
+        transform("re", 0, 0)
+        transform("re", 0, 1)
+        transform("im", 1, 0)
+        transform("re", 1, 1)
+        add_squares(0, 0, 0, 512)
+        add_squares(0, 1, 0, 512)
+        add_squares(1, 0, 0, 512)
+        quantise_power(0, 0, 0, 512)
+        load_filters()
+        transform("im", 1, 1, 2)
+        cast_filters()
+        quantise_power(1, 0, 0, 512)
+        quantise_filters()
+        filter_bank(0, 512, "scalar")
+        add_squares(1, 1, 256, 256)
+        quantise_power(1, 1, 256, 256)
+        add_squares(1, 1, 0, 256)
+        quantise_power(0, 1, 0, 512)
+        filter_bank(768, 256, "both")
+        quantise_power(1, 1, 0, 256)
+        filter_bank(512, 256, "both")

@@ -27,17 +27,15 @@ def tile_list_meltab_pow_kernel(tc, tab_words, tab_scales, co, si, gn, fb, offs,
     nc = tc.nc
     with ExitStack() as ctx:
         keep = ctx.enter_context(tc.tile_pool(name="keep", bufs=1))
-        raws = ctx.enter_context(tc.tile_pool(name="raws", bufs=4))
-        casts = ctx.enter_context(tc.tile_pool(name="casts", bufs=4))
+        raws = ctx.enter_context(tc.tile_pool(name="raws", bufs=5))
         squares = ctx.enter_context(tc.tile_pool(name="squares", bufs=3))
-        powers = ctx.enter_context(tc.tile_pool(name="powers", bufs=3))
-        results = ctx.enter_context(tc.tile_pool(name="results", bufs=3))
-        psum = ctx.enter_context(tc.psum_pool(name="psum", bufs=8))
+        results = ctx.enter_context(tc.tile_pool(name="results", bufs=4))
+        psum = ctx.enter_context(tc.psum_pool(name="psum", bufs=1))
 
         offsets = keep.tile([P, J // 16], U16, name="offsets")
         nc.sync.dma_start(offsets[:], offs)
 
-        scale_store = keep.tile([P, T // 4], I32, name="w_codes_re00", align_bytes=64)
+        scale_store = keep.tile([P, T // 4], I32, name="ss", align_bytes=64)
         nc.gpsimd.memset(scale_store[:], 0)
         scale_rows = tab_scales.bitcast(I32)
 
@@ -57,8 +55,8 @@ def tile_list_meltab_pow_kernel(tc, tab_words, tab_scales, co, si, gn, fb, offs,
             nc.sync.dma_start(out=tile[:], in_=rows.rearrange("(p i) f -> p i f", i=PACK))
             raw[part, a, g] = tile
 
-        def cast(part, a, g, engine):
-            tile = casts.tile([P, PACK * BANK], BF16, name="grouped", align_bytes=64)
+        def cast(part, a, g, engine, slot):
+            tile = keep.tile([P, PACK * BANK], BF16, name=slot, align_bytes=64)
             dst = tile[:].rearrange("p (t m i) -> p m i t", t=PACK, i=PACK)
             src = raw[part, a, g][:].rearrange("p i (m t) -> p m i t", t=PACK)
             if engine == "scalar":
@@ -70,8 +68,8 @@ def tile_list_meltab_pow_kernel(tc, tab_words, tab_scales, co, si, gn, fb, offs,
                 nc.vector.tensor_copy(out=dst, in_=src)
             grouped[part, a, g] = tile
 
-        def quantise_weight(part, a, g):
-            codes = keep.tile([P, BANK], U32, name="w_codes_%s%d%d" % (part, a, g), align_bytes=64)
+        def quantise_weight(part, a, g, slot):
+            codes = keep.tile([P, BANK], U32, name=slot, align_bytes=64)
             scales = keep.tile([P, BANK], U8, name="w_scales_%s%d%d" % (part, a, g), align_bytes=64)
             nc.vector.quantize_mx(out=codes[:].bitcast(FP8X4), scales=scales[:], in_=grouped[part, a, g][:])
             w_codes[part, a, g], w_scales[part, a, g] = codes, scales
@@ -88,10 +86,10 @@ def tile_list_meltab_pow_kernel(tc, tab_words, tab_scales, co, si, gn, fb, offs,
             window = scale_store[:].bitcast(U8)
             nc.vector.tensor_copy(picked_scales[0][:], window.indirect(offsets[:]))
             nc.gpsimd.memset(picked_scales[1][:].bitcast(I32), 0)
-            nc.scalar.dma_start(out=picked_scales[1][0:112, :].bitcast(I32), in_=picked_scales[0][4:116, :].bitcast(I32))
+            nc.sync.dma_start(out=picked_scales[1][0:112, :].bitcast(I32), in_=picked_scales[0][4:116, :].bitcast(I32))
 
-        def gather_words(h):
-            picked_words[h] = keep.tile([P, BANK], U32, name="picked_words", align_bytes=64)
+        def gather_words(h, slot):
+            picked_words[h] = keep.tile([P, BANK], U32, name=slot, align_bytes=64)
             window = word_store[:].bitcast(U32)
             nc.vector.tensor_copy(picked_words[h][:], window.indirect(offsets[:, 32 * h : 32 * (h + 1)]))
 
@@ -123,11 +121,11 @@ def tile_list_meltab_pow_kernel(tc, tab_words, tab_scales, co, si, gn, fb, offs,
             nc.vector.tensor_tensor(out=total[:], in0=ratio[:], in1=guess[:], op=ALU.add)
             nc.vector.tensor_scalar(out=root[:], in0=total[:], scalar1=0.5, scalar2=None, op0=ALU.mult)
 
-        def transform(part, g, h, pieces=1):
+        def transform(part, g, h, first, pieces):
             tile = squares.tile([P, PACK, BANK], F32, name="squared_" + part, align_bytes=64)
             banks = []
             for t in range(PACK):
-                bank = psum.tile([P, BANK], F32, name="bank")
+                bank = psum.tile([P, BANK], F32, name="bank%d" % (first + t))
                 cols = slice(t * P, (t + 1) * P)
                 for a in range(2):
                     nc.tensor.matmul_mx(
@@ -152,8 +150,8 @@ def tile_list_meltab_pow_kernel(tc, tab_words, tab_scales, co, si, gn, fb, offs,
         h_scales = [keep.tile([P, J], U8, name="h_scales%d" % g, align_bytes=64) for g in range(2)]
         power = {}
 
-        def add_squares(g, h, lo, width):
-            tile = powers.tile([P, PACK * BANK], BF16, name="power", align_bytes=64)
+        def add_squares(g, h, lo, width, slot):
+            tile = keep.tile([P, PACK * width], BF16, name=slot, align_bytes=64)
             cols = slice(lo, lo + width)
             nc.vector.tensor_tensor(
                 out=tile[:, : PACK * width].rearrange("p (c i t) -> p c t i", i=4, t=PACK),
@@ -167,39 +165,39 @@ def tile_list_meltab_pow_kernel(tc, tab_words, tab_scales, co, si, gn, fb, offs,
             cols = slice(h * BANK + lo, h * BANK + lo + width)
             nc.vector.quantize_mx(out=h_codes[g][:, cols].bitcast(FP8X4), scales=h_scales[g][:, cols], in_=power[g, h, lo][:, : PACK * width])
 
-        fb_codes = keep.tile([P, 2 * N], U32, name="fb_codes", align_bytes=64)
-        fb_scales = keep.tile([P, 2 * N], U8, name="fb_scales", align_bytes=64)
+        fb_codes, fb_scales = {}, {}
 
-        def load_filters():
-            tile = raws.tile([P, 2, PACK, N], F32, name="raw", align_bytes=64)
-            nc.sync.dma_start(out=tile[:], in_=fb.rearrange("(g p t) n -> p g t n", g=2, t=PACK))
-            raw["fb"] = tile
+        def load_filters(g):
+            tile = keep.tile([P, PACK, N], F32, name="fb_raw%d" % g, align_bytes=64)
+            nc.sync.dma_start(out=tile[:], in_=fb[g * PASS : (g + 1) * PASS, :].rearrange("(p t) n -> p t n", t=PACK))
+            raw["fb", g] = tile
 
-        def cast_filters():
-            tile = casts.tile([P, 2, PACK * N], BF16, name="grouped", align_bytes=64)
-            for g in range(2):
-                nc.vector.tensor_tensor(
-                    out=tile[:, g, :].rearrange("p (c i t) -> p c t i", i=4, t=PACK),
-                    in0=raw["fb"][:, g, :, :].rearrange("p t (c i) -> p c t i", i=4),
-                    in1=sign[:, g, :].unsqueeze(1).unsqueeze(3).to_broadcast([P, N // 4, PACK, 4]),
-                    op=ALU.mult,
-                )
-            grouped["fb"] = tile
+        def cast_filters(g, slot):
+            tile = keep.tile([P, PACK * N], BF16, name=slot, align_bytes=64)
+            nc.vector.tensor_tensor(
+                out=tile[:].rearrange("p (c i t) -> p c t i", i=4, t=PACK),
+                in0=raw["fb", g][:].rearrange("p t (c i) -> p c t i", i=4),
+                in1=sign[:, g, :].unsqueeze(1).unsqueeze(3).to_broadcast([P, N // 4, PACK, 4]),
+                op=ALU.mult,
+            )
+            grouped["fb", g] = tile
 
-        def quantise_filters():
-            nc.vector.quantize_mx(out=fb_codes[:].bitcast(FP8X4), scales=fb_scales[:], in_=grouped["fb"][:].rearrange("p g w -> p (g w)"))
+        def quantise_filters(g, slot):
+            fb_codes[g] = keep.tile([P, N], U32, name=slot, align_bytes=64)
+            fb_scales[g] = keep.tile([P, N], U8, name="fb_scales%d" % g, align_bytes=64)
+            nc.vector.quantize_mx(out=fb_codes[g][:].bitcast(FP8X4), scales=fb_scales[g][:], in_=grouped["fb", g][:])
 
-        def filter_bank(lo, width, engine):
+        def filter_bank(lo, width, first, engine):
             frames_cols = slice(lo, lo + width)
             result = results.tile([P, 2, BANK], F32, name="result", align_bytes=64)
             for b in range(2):
-                bank = psum.tile([P, BANK], F32, name="bank")
+                bank = psum.tile([P, BANK], F32, name="bank%d" % (first + b))
                 for g in range(2):
-                    cols = slice(g * N + b * P, g * N + (b + 1) * P)
+                    cols = slice(b * P, (b + 1) * P)
                     nc.tensor.matmul_mx(
                         out=bank[:, :width],
-                        lhsT=fb_codes[:, cols].bitcast(FP8X4),
-                        lhsT_scale=fb_scales[:, cols],
+                        lhsT=fb_codes[g][:, cols].bitcast(FP8X4),
+                        lhsT_scale=fb_scales[g][:, cols],
                         rhs=h_codes[g][:, frames_cols].bitcast(FP8X4),
                         rhs_scale=h_scales[g][:, frames_cols],
                         start=(g == 0),
@@ -211,59 +209,65 @@ def tile_list_meltab_pow_kernel(tc, tab_words, tab_scales, co, si, gn, fb, offs,
                     nc.vector.tensor_copy(out=result[:, b, :width], in_=bank[:, :width])
             nc.sync.dma_start(out=out.rearrange("(b p) j -> p b j", p=P)[:, :, frames_cols], in_=result[:, :, :width])
 
-        load_scales()
+        prepare_gain()
         load("re", 0, 0)
+        load_scales()
         load_table()
         load("re", 1, 0)
         gather_scales()
-        gather_words(0)
-        load("im", 1, 0)
         load("im", 0, 0)
-        cast("im", 1, 0, "vector")
-        cast("im", 0, 0, "vector")
+        cast("re", 0, 0, "scalar", "grpre00")
+        load("im", 1, 0)
+        quantise_weight("re", 0, 0, "ss")
+        gather_words(0, "pw0")
         part_words(0)
-        cast("re", 0, 0, "split")
-        cast("re", 1, 0, "split")
+        cast("re", 1, 0, "scalar", "grpre10")
         load("re", 0, 1)
-        load("re", 1, 1)
-        cast("re", 1, 1, "vector")
-        quantise_weight("im", 1, 0)
-        prepare_gain()
-        quantise_weight("im", 0, 0)
-        cast("re", 0, 1, "vector")
-        quantise_weight("re", 1, 1)
-        quantise_weight("re", 0, 0)
-        quantise_weight("re", 1, 0)
-        load("im", 0, 1)
-        cast("im", 0, 1, "scalar")
-        load("im", 1, 1)
-        gather_words(1)
-        transform("im", 0, 0)
+        gather_words(1, "pw0")
+        quantise_weight("re", 1, 0, "wre10")
         part_words(1)
-        cast("im", 1, 1, "split")
-        quantise_weight("re", 0, 1)
-        transform("im", 0, 1)
-        quantise_weight("im", 1, 1)
-        quantise_weight("im", 0, 1)
-        transform("re", 1, 0)
-        transform("re", 0, 0)
-        transform("re", 0, 1)
-        transform("im", 1, 0)
-        transform("re", 1, 1)
-        add_squares(0, 0, 0, 512)
-        add_squares(0, 1, 0, 512)
-        add_squares(1, 0, 0, 512)
+        transform("re", 0, 0, 0, 1)
+        cast("im", 0, 0, "vector", "grpim00")
+        load("re", 1, 1)
+        cast("im", 1, 0, "vector", "grpim10")
+        load("im", 0, 1)
+        quantise_weight("im", 0, 0, "wim00")
+        quantise_weight("im", 1, 0, "wim10")
+        transform("re", 0, 1, 4, 1)
+        transform("im", 0, 0, 0, 1)
+        cast("re", 0, 1, "vector", "grpre01")
+        load("im", 1, 1)
+        quantise_weight("re", 0, 1, "wre01")
+        cast("re", 1, 1, "vector", "grpre11")
+        load_filters(0)
+        load_filters(1)
+        quantise_weight("re", 1, 1, "wre11")
+        transform("im", 0, 1, 4, 1)
+        cast("im", 0, 1, "scalar", "grpim01")
+        add_squares(0, 0, 0, 512, "grpre11")
+        cast("im", 1, 1, "vector", "grpim11")
+        quantise_weight("im", 0, 1, "wim01")
+        quantise_weight("im", 1, 1, "wim11")
         quantise_power(0, 0, 0, 512)
-        load_filters()
-        transform("im", 1, 1, 2)
-        cast_filters()
-        quantise_power(1, 0, 0, 512)
-        quantise_filters()
-        filter_bank(0, 512, "scalar")
-        add_squares(1, 1, 256, 256)
-        quantise_power(1, 1, 256, 256)
-        add_squares(1, 1, 0, 256)
+        transform("re", 1, 0, 0, 1)
+        transform("re", 1, 1, 4, 1)
+        add_squares(0, 1, 0, 512, "grpim11")
+        cast_filters(0, "grpfb0")
+        cast_filters(1, "grpfb1")
         quantise_power(0, 1, 0, 512)
-        filter_bank(768, 256, "both")
+        quantise_filters(0, "wfb0")
+        quantise_filters(1, "wfb1")
+        transform("im", 1, 0, 0, 2)
+        add_squares(1, 0, 0, 256, "pow10_0")
+        add_squares(1, 0, 256, 256, "pow10_256")
+        quantise_power(1, 0, 0, 256)
+        transform("im", 1, 1, 4, 2)
+        filter_bank(0, 256, 0, "scalar")
+        quantise_power(1, 0, 256, 256)
+        add_squares(1, 1, 0, 256, "pow11_0")
+        filter_bank(256, 256, 2, "scalar")
         quantise_power(1, 1, 0, 256)
-        filter_bank(512, 256, "both")
+        add_squares(1, 1, 256, 256, "pow11_256")
+        filter_bank(512, 256, 0, "scalar")
+        quantise_power(1, 1, 256, 256)
+        filter_bank(768, 256, 2, "both")

@@ -29,11 +29,13 @@ def tile_list_meltab_pow_kernel(tc, tab_words, tab_scales, co, si, gn, fb, offs,
         keep = ctx.enter_context(tc.tile_pool(name="keep", bufs=1))
         raws = ctx.enter_context(tc.tile_pool(name="raws", bufs=5))
         squares = ctx.enter_context(tc.tile_pool(name="squares", bufs=3))
-        results = ctx.enter_context(tc.tile_pool(name="results", bufs=4))
+        results = ctx.enter_context(tc.tile_pool(name="results", bufs=5))
         psum = ctx.enter_context(tc.psum_pool(name="psum", bufs=1))
 
         offsets = keep.tile([P, J // 16], U16, name="offsets")
-        nc.sync.dma_start(offsets[:], offs)
+
+        def load_offsets():
+            nc.sync.dma_start(offsets[:], offs)
 
         scale_store = keep.tile([P, T // 4], I32, name="ss", align_bytes=64)
         nc.gpsimd.memset(scale_store[:], 0)
@@ -44,7 +46,9 @@ def tile_list_meltab_pow_kernel(tc, tab_words, tab_scales, co, si, gn, fb, offs,
                 nc.sync.dma_start(out=scale_store[32 * q : 32 * q + 8, :], in_=scale_rows[:, 4 * q : 4 * q + 4, :])
 
         gain = keep.tile([P, 2, PACK], F32, name="gain")
-        nc.sync.dma_start(out=gain[:], in_=gn.rearrange("(g p t) -> p g t", g=2, t=PACK))
+
+        def load_gain():
+            nc.sync.dma_start(out=gain[:], in_=gn.rearrange("(g p t) -> p g t", g=2, t=PACK))
 
         weights = {"re": co, "im": si}
         raw, grouped, w_codes, w_scales, squared = {}, {}, {}, {}, {}
@@ -121,21 +125,21 @@ def tile_list_meltab_pow_kernel(tc, tab_words, tab_scales, co, si, gn, fb, offs,
             nc.vector.tensor_tensor(out=total[:], in0=ratio[:], in1=guess[:], op=ALU.add)
             nc.vector.tensor_scalar(out=root[:], in0=total[:], scalar1=0.5, scalar2=None, op0=ALU.mult)
 
-        def transform(part, g, h, first, pieces):
+        def transform(part, g, h, first, pieces, lead):
             tile = squares.tile([P, PACK, BANK], F32, name="squared_" + part, align_bytes=64)
             banks = []
             for t in range(PACK):
                 bank = psum.tile([P, BANK], F32, name="bank%d" % (first + t))
                 cols = slice(t * P, (t + 1) * P)
-                for a in range(2):
+                for a in (lead, 1 - lead):
                     nc.tensor.matmul_mx(
                         out=bank[:],
                         lhsT=w_codes[part, a, g][:, cols].bitcast(FP8X4),
                         lhsT_scale=w_scales[part, a, g][:, cols],
                         rhs=frames[h][:, a, :].bitcast(FP4X4),
                         rhs_scale=picked_scales[a][:, h * BANK : (h + 1) * BANK],
-                        start=(a == 0),
-                        stop=(a == 1),
+                        start=(a == lead),
+                        stop=(a != lead),
                     )
                 banks.append(bank)
             width = BANK // pieces
@@ -154,9 +158,9 @@ def tile_list_meltab_pow_kernel(tc, tab_words, tab_scales, co, si, gn, fb, offs,
             tile = keep.tile([P, PACK * width], BF16, name=slot, align_bytes=64)
             cols = slice(lo, lo + width)
             nc.vector.tensor_tensor(
-                out=tile[:, : PACK * width].rearrange("p (c i t) -> p c t i", i=4, t=PACK),
-                in0=squared["re", g, h][:, :, cols].rearrange("p t (c i) -> p c t i", i=4),
-                in1=squared["im", g, h][:, :, cols].rearrange("p t (c i) -> p c t i", i=4),
+                out=tile[:, : PACK * width].rearrange("p (c i t) -> p c t i", i=2, t=PACK),
+                in0=squared["re", g, h][:, :, cols].rearrange("p t (c i) -> p c t i", i=2),
+                in1=squared["im", g, h][:, :, cols].rearrange("p t (c i) -> p c t i", i=2),
                 op=ALU.add,
             )
             power[g, h, lo] = tile
@@ -175,9 +179,9 @@ def tile_list_meltab_pow_kernel(tc, tab_words, tab_scales, co, si, gn, fb, offs,
         def cast_filters(g, slot):
             tile = keep.tile([P, PACK * N], BF16, name=slot, align_bytes=64)
             nc.vector.tensor_tensor(
-                out=tile[:].rearrange("p (c i t) -> p c t i", i=4, t=PACK),
-                in0=raw["fb", g][:].rearrange("p t (c i) -> p c t i", i=4),
-                in1=sign[:, g, :].unsqueeze(1).unsqueeze(3).to_broadcast([P, N // 4, PACK, 4]),
+                out=tile[:].rearrange("p (c i t) -> p c t i", i=2, t=PACK),
+                in0=raw["fb", g][:].rearrange("p t (c i) -> p c t i", i=2),
+                in1=sign[:, g, :].unsqueeze(1).unsqueeze(3).to_broadcast([P, N // 2, PACK, 2]),
                 op=ALU.mult,
             )
             grouped["fb", g] = tile
@@ -209,12 +213,14 @@ def tile_list_meltab_pow_kernel(tc, tab_words, tab_scales, co, si, gn, fb, offs,
                     nc.vector.tensor_copy(out=result[:, b, :width], in_=bank[:, :width])
             nc.sync.dma_start(out=out.rearrange("(b p) j -> p b j", p=P)[:, :, frames_cols], in_=result[:, :, :width])
 
-        prepare_gain()
         load("re", 0, 0)
+        load_offsets()
         load_scales()
+        load_gain()
         load_table()
         load("re", 1, 0)
         gather_scales()
+        prepare_gain()
         load("im", 0, 0)
         cast("re", 0, 0, "scalar", "grpre00")
         load("im", 1, 0)
@@ -226,48 +232,51 @@ def tile_list_meltab_pow_kernel(tc, tab_words, tab_scales, co, si, gn, fb, offs,
         gather_words(1, "pw0")
         quantise_weight("re", 1, 0, "wre10")
         part_words(1)
-        transform("re", 0, 0, 0, 1)
+        transform("re", 0, 0, 0, 1, 0)
         cast("im", 0, 0, "vector", "grpim00")
         load("re", 1, 1)
         cast("im", 1, 0, "vector", "grpim10")
+        load_filters(0)
         load("im", 0, 1)
         quantise_weight("im", 0, 0, "wim00")
         quantise_weight("im", 1, 0, "wim10")
-        transform("re", 0, 1, 4, 1)
-        transform("im", 0, 0, 0, 1)
+        transform("re", 0, 1, 4, 1, 1)
+        transform("im", 0, 0, 0, 1, 0)
         cast("re", 0, 1, "vector", "grpre01")
         load("im", 1, 1)
         quantise_weight("re", 0, 1, "wre01")
         cast("re", 1, 1, "vector", "grpre11")
-        load_filters(0)
         load_filters(1)
         quantise_weight("re", 1, 1, "wre11")
-        transform("im", 0, 1, 4, 1)
+        cast_filters(0, "grpfb0")
+        transform("im", 0, 1, 4, 1, 1)
         cast("im", 0, 1, "scalar", "grpim01")
         add_squares(0, 0, 0, 512, "grpre11")
         cast("im", 1, 1, "vector", "grpim11")
         quantise_weight("im", 0, 1, "wim01")
         quantise_weight("im", 1, 1, "wim11")
         quantise_power(0, 0, 0, 512)
-        transform("re", 1, 0, 0, 1)
-        transform("re", 1, 1, 4, 1)
+        transform("re", 1, 0, 0, 1, 0)
+        transform("re", 1, 1, 4, 1, 1)
         add_squares(0, 1, 0, 512, "grpim11")
-        cast_filters(0, "grpfb0")
         cast_filters(1, "grpfb1")
         quantise_power(0, 1, 0, 512)
         quantise_filters(0, "wfb0")
         quantise_filters(1, "wfb1")
-        transform("im", 1, 0, 0, 2)
+        transform("im", 1, 0, 0, 2, 0)
         add_squares(1, 0, 0, 256, "pow10_0")
         add_squares(1, 0, 256, 256, "pow10_256")
         quantise_power(1, 0, 0, 256)
-        transform("im", 1, 1, 4, 2)
+        transform("im", 1, 1, 4, 2, 1)
         filter_bank(0, 256, 0, "scalar")
         quantise_power(1, 0, 256, 256)
         add_squares(1, 1, 0, 256, "pow11_0")
         filter_bank(256, 256, 2, "scalar")
         quantise_power(1, 1, 0, 256)
-        add_squares(1, 1, 256, 256, "pow11_256")
+        add_squares(1, 1, 256, 128, "pow11_256")
         filter_bank(512, 256, 0, "scalar")
-        quantise_power(1, 1, 256, 256)
-        filter_bank(768, 256, 2, "both")
+        quantise_power(1, 1, 256, 128)
+        add_squares(1, 1, 384, 128, "pow11_384")
+        filter_bank(768, 128, 2, "scalar")
+        quantise_power(1, 1, 384, 128)
+        filter_bank(896, 128, 0, "both")

@@ -42,8 +42,8 @@ def tile_list_meltab_pow_kernel(tc, tab_words, tab_scales, co, si, gn, fb, offs,
         scale_rows = tab_scales.bitcast(I32)
 
         def load_scales():
-            for q in range(4):
-                nc.sync.dma_start(out=scale_store[32 * q : 32 * q + 8, :], in_=scale_rows[:, 4 * q : 4 * q + 4, :])
+            for r in range(4):
+                nc.sync.dma_start(out=scale_store[r:P:16, :], in_=scale_rows.rearrange("a (q r) t -> r q a t", r=4)[r])
 
         gain = keep.tile([P, 2, PACK], F32, name="gain")
 
@@ -90,7 +90,7 @@ def tile_list_meltab_pow_kernel(tc, tab_words, tab_scales, co, si, gn, fb, offs,
             window = scale_store[:].bitcast(U8)
             nc.vector.tensor_copy(picked_scales[0][:], window.indirect(offsets[:]))
             nc.gpsimd.memset(picked_scales[1][:].bitcast(I32), 0)
-            nc.sync.dma_start(out=picked_scales[1][0:112, :].bitcast(I32), in_=picked_scales[0][4:116, :].bitcast(I32))
+            nc.sync.dma_start(out=picked_scales[1][0:112, :].bitcast(I32), in_=picked_scales[0][16:128, :].bitcast(I32))
 
         def gather_words(h, slot):
             picked_words[h] = keep.tile([P, BANK], U32, name=slot, align_bytes=64)

@@ -27,138 +27,137 @@ def tile_list_meltab_pow_kernel(tc, tab_words, tab_scales, co, si, gn, fb, offs,
     nc = tc.nc
     with ExitStack() as ctx:
         keep = ctx.enter_context(tc.tile_pool(name="keep", bufs=1))
-        raws = ctx.enter_context(tc.tile_pool(name="raws", bufs=5))
-        squares = ctx.enter_context(tc.tile_pool(name="squares", bufs=3))
-        results = ctx.enter_context(tc.tile_pool(name="results", bufs=5))
         psum = ctx.enter_context(tc.psum_pool(name="psum", bufs=1))
 
+        def sbuf(shape, dtype, slot):
+            return keep.tile(shape, dtype, name=slot, align_bytes=64)
+
         offsets = keep.tile([P, J // 16], U16, name="offsets")
+        scale_store = sbuf([P, T // 4], I32, "scale_store")
+        word_store = sbuf([P, T], I32, "word_store")
+        picked_scales = sbuf([P, J], U8, "picked_scales")
+        planes = sbuf([P, 2 * J], U8, "planes")
+        picked_words = [sbuf([P, BANK], U32, "picked_words%d" % h) for h in range(2)]
+        frames = {}
+        gain = keep.tile([P, 2, 2 * PACK], F32, name="gain")
+        root = keep.tile([P, 2 * PACK], F32, name="root")
+        sign = keep.tile([P, 2, PACK], F32, name="sign")
+        weights = {"re": co, "im": si}
+        raw, grouped, w_codes, w_scales, squared, power = {}, {}, {}, {}, {}, {}
+        fb_codes, fb_scales = {}, {}
+        h_codes = [sbuf([P, J], U32, "h_codes%d" % g) for g in range(2)]
+        h_scales = [sbuf([P, J], U8, "h_scales%d" % g) for g in range(2)]
 
-        def load_offsets():
-            nc.sync.dma_start(offsets[:], offs)
-
-        scale_store = keep.tile([P, T // 4], I32, name="ss", align_bytes=64)
-        nc.gpsimd.memset(scale_store[:], 0)
-        scale_rows = tab_scales.bitcast(I32)
+        def load_table(lo, hi):
+            words = tab_words[0].rearrange("p t b -> p (t b)").bitcast(I32)
+            nc.sync.dma_start(out=word_store[:, lo:hi], in_=words[:, lo:hi])
 
         def load_scales():
-            for r in range(4):
-                nc.sync.dma_start(out=scale_store[r:P:16, :], in_=scale_rows.rearrange("a (q r) t -> r q a t", r=4)[r])
-
-        gain = keep.tile([P, 2, PACK], F32, name="gain")
+            rows = tab_scales.bitcast(I32).rearrange("a q t -> q a t")
+            nc.sync.dma_start(out=scale_store[0:P:4, :], in_=rows)
 
         def load_gain():
-            nc.sync.dma_start(out=gain[:], in_=gn.rearrange("(g p t) -> p g t", g=2, t=PACK))
-
-        weights = {"re": co, "im": si}
-        raw, grouped, w_codes, w_scales, squared = {}, {}, {}, {}, {}
+            runs = gn.rearrange("(g q e) -> q g e", g=2, e=2 * PACK)
+            for r in range(2):
+                nc.sync.dma_start(out=gain[r:P:2, :, :7], in_=runs[:, :, r : r + 7])
 
         def load(part, a, g):
-            tile = raws.tile([P, PACK, BANK], F32, name="raw", align_bytes=64)
+            tile = sbuf([P, PACK, BANK], F32, "raw_%s%d%d" % (part, a, g))
             rows = weights[part][a * PASS : (a + 1) * PASS, g * BANK : (g + 1) * BANK]
             nc.sync.dma_start(out=tile[:], in_=rows.rearrange("(p i) f -> p i f", i=PACK))
             raw[part, a, g] = tile
 
-        def cast(part, a, g, engine, slot):
-            tile = keep.tile([P, PACK * BANK], BF16, name=slot, align_bytes=64)
-            dst = tile[:].rearrange("p (t m i) -> p m i t", t=PACK, i=PACK)
-            src = raw[part, a, g][:].rearrange("p i (m t) -> p m i t", t=PACK)
-            if engine == "scalar":
-                nc.scalar.copy(out=dst, in_=src)
-            elif engine == "split":
-                nc.vector.tensor_copy(out=dst[:, : P // 2], in_=src[:, : P // 2])
-                nc.scalar.copy(out=dst[:, P // 2 :], in_=src[:, P // 2 :])
-            else:
-                nc.vector.tensor_copy(out=dst, in_=src)
-            grouped[part, a, g] = tile
+        def load_filters(g):
+            tile = sbuf([P, PACK, N], F32, "fb_raw%d" % g)
+            rows = fb[g * PASS : (g + 1) * PASS, :].rearrange("(q t r) n -> r q t n", t=PACK, r=2)
+            for r in range(2):
+                nc.sync.dma_start(out=tile[r:P:2], in_=rows[r])
+            raw["fb", g] = tile
 
-        def quantise_weight(part, a, g, slot):
-            codes = keep.tile([P, BANK], U32, name=slot, align_bytes=64)
-            scales = keep.tile([P, BANK], U8, name="w_scales_%s%d%d" % (part, a, g), align_bytes=64)
-            nc.vector.quantize_mx(out=codes[:].bitcast(FP8X4), scales=scales[:], in_=grouped[part, a, g][:])
-            w_codes[part, a, g], w_scales[part, a, g] = codes, scales
-
-        word_store = keep.tile([P, T], I32, name="word_store", align_bytes=64)
-        picked_scales = [keep.tile([P, J], U8, name="picked_scales%d" % a, align_bytes=64) for a in range(2)]
-        picked_words = {}
-        frames = [keep.tile([P, 2, 2 * BANK], U8, name="frames%d" % h, align_bytes=64) for h in range(2)]
-
-        def load_table():
-            nc.sync.dma_start(out=word_store[:], in_=tab_words[0].rearrange("p t b -> p (t b)").bitcast(I32))
+        def prepare_gain():
+            flat = gain[:].rearrange("p g (t r) -> p (g t) r", r=2)[:, :, 0]
+            flat_sign = sign[:].rearrange("p g t -> p (g t)")
+            twice = keep.tile([P, 2 * PACK], F32, name="twice")
+            size = keep.tile([P, 2 * PACK], F32, name="size")
+            half = keep.tile([P, 2 * PACK], F32, name="half")
+            nc.gpsimd.memset(half[:], 0.5)
+            nc.gpsimd.tensor_scalar(out=twice[:], in0=flat, scalar1=0.0, scalar2=2.0, op0=ALU.is_ge, op1=ALU.mult)
+            nc.gpsimd.tensor_scalar(out=flat_sign, in0=twice[:], scalar1=-1.0, scalar2=None, op0=ALU.add)
+            nc.gpsimd.tensor_tensor(out=size[:], in0=flat, in1=flat_sign, op=ALU.mult)
+            nc.gpsimd.tensor_tensor(out=root[:], in0=size[:], in1=half[:], op=ALU.pow)
 
         def gather_scales():
-            window = scale_store[:].bitcast(U8)
-            nc.vector.tensor_copy(picked_scales[0][:], window.indirect(offsets[:]))
-            nc.gpsimd.memset(picked_scales[1][:].bitcast(I32), 0)
-            nc.sync.dma_start(out=picked_scales[1][0:112, :].bitcast(I32), in_=picked_scales[0][16:128, :].bitcast(I32))
+            nc.vector.tensor_copy(picked_scales[:], scale_store[:].bitcast(U8).indirect(offsets[:]))
+            for q in (0, 2, 1, 3):
+                nc.sync.dma_start(out=planes[32 * q : 32 * q + 4, :].bitcast(I32), in_=picked_scales[32 * q : 32 * (q + 1) : 4, :].bitcast(I32))
 
-        def gather_words(h, slot):
-            picked_words[h] = keep.tile([P, BANK], U32, name=slot, align_bytes=64)
+        def gather_words(h):
             window = word_store[:].bitcast(U32)
             nc.vector.tensor_copy(picked_words[h][:], window.indirect(offsets[:, 32 * h : 32 * (h + 1)]))
 
-        def part_words(h):
+        def part_words(h, slot):
+            frames[h] = sbuf([P, 2, 2 * BANK], U8, slot)
             nc.vector.tensor_copy(
                 out=frames[h][:].bitcast(U16),
                 in_=picked_words[h][:].bitcast(U16).rearrange("p (j a) -> p a j", a=2),
             )
 
-        root = keep.tile([P, 2 * PACK], F32, name="root")
-        sign = keep.tile([P, 2, PACK], F32, name="sign")
+        def cast(part, a, g, first, count, engine):
+            tile = sbuf([P, count * BANK], BF16, "grouped_%s%d%d%d" % (part, a, g, first))
+            dst = tile[:].rearrange("p (t q r i) -> p t q i r", t=count, r=2, i=PACK)
+            src = raw[part, a, g][:].rearrange("p i (q t r) -> p t q i r", t=PACK, r=2)[:, first : first + count]
+            if engine == "scalar":
+                nc.scalar.copy(out=dst, in_=src)
+            else:
+                nc.vector.tensor_copy(out=dst, in_=src)
+            for t in range(count):
+                grouped[part, a, g, first + t] = (tile, t)
 
-        def prepare_gain():
-            flat = gain[:].rearrange("p g t -> p (g t)")
-            size = keep.tile([P, 2 * PACK], F32, name="size")
-            guess = keep.tile([P, 2 * PACK], F32, name="guess")
-            safe = keep.tile([P, 2 * PACK], F32, name="safe")
-            inverse = keep.tile([P, 2 * PACK], F32, name="inverse")
-            ratio = keep.tile([P, 2 * PACK], F32, name="ratio")
-            total = keep.tile([P, 2 * PACK], F32, name="total")
-            twice = keep.tile([P, 2 * PACK], F32, name="twice")
-            nc.vector.scalar_tensor_tensor(out=size[:], in0=flat, scalar=-1.0, in1=flat, op0=ALU.mult, op1=ALU.max)
-            nc.scalar.activation(out=guess[:], in_=size[:], func=ACT.Sqrt)
-            nc.vector.tensor_scalar(out=twice[:], in0=flat, scalar1=0.0, scalar2=2.0, op0=ALU.is_ge, op1=ALU.mult)
-            nc.vector.tensor_scalar(out=sign[:].rearrange("p g t -> p (g t)"), in0=twice[:], scalar1=-1.0, scalar2=None, op0=ALU.add)
-            nc.vector.tensor_scalar(out=safe[:], in0=guess[:], scalar1=TINY, scalar2=None, op0=ALU.max)
-            nc.vector.reciprocal(out=inverse[:], in_=safe[:])
-            nc.vector.tensor_tensor(out=ratio[:], in0=size[:], in1=inverse[:], op=ALU.mult)
-            nc.vector.tensor_tensor(out=total[:], in0=ratio[:], in1=guess[:], op=ALU.add)
-            nc.vector.tensor_scalar(out=root[:], in0=total[:], scalar1=0.5, scalar2=None, op0=ALU.mult)
-
-        def transform(part, g, h, first, pieces, lead):
-            tile = squares.tile([P, PACK, BANK], F32, name="squared_" + part, align_bytes=64)
-            banks = []
-            for t in range(PACK):
-                bank = psum.tile([P, BANK], F32, name="bank%d" % (first + t))
+        def quantise_weight(part, a, g, first, count, slot=None):
+            name = "%s%d%d%d" % (part, a, g, first)
+            codes = sbuf([P, count * P], U32, slot or "w_codes_" + name)
+            scales = sbuf([P, count * P], U8, "w_scales_" + name)
+            tile, t = grouped[part, a, g, first]
+            nc.vector.quantize_mx(out=codes[:].bitcast(FP8X4), scales=scales[:], in_=tile[:, t * BANK : (t + count) * BANK])
+            for t in range(count):
                 cols = slice(t * P, (t + 1) * P)
-                for a in (lead, 1 - lead):
-                    nc.tensor.matmul_mx(
-                        out=bank[:],
-                        lhsT=w_codes[part, a, g][:, cols].bitcast(FP8X4),
-                        lhsT_scale=w_scales[part, a, g][:, cols],
-                        rhs=frames[h][:, a, :].bitcast(FP4X4),
-                        rhs_scale=picked_scales[a][:, h * BANK : (h + 1) * BANK],
-                        start=(a == lead),
-                        stop=(a != lead),
-                    )
-                banks.append(bank)
-            width = BANK // pieces
-            for c in range(pieces):
-                cols = slice(c * width, (c + 1) * width)
-                for t in range(PACK):
-                    column = PACK * g + t
-                    nc.scalar.activation(out=tile[:, t, cols], in_=banks[t][:, cols], func=ACT.Square, scale=root[:, column : column + 1])
-            squared[part, g, h] = tile
+                w_codes[part, a, g, first + t], w_scales[part, a, g, first + t] = codes[:, cols], scales[:, cols]
 
-        h_codes = [keep.tile([P, J], U32, name="h_codes%d" % g, align_bytes=64) for g in range(2)]
-        h_scales = [keep.tile([P, J], U8, name="h_scales%d" % g, align_bytes=64) for g in range(2)]
-        power = {}
+        sums = {}
+
+        def transform(part, g, h, t, bank, lead):
+            sums[t] = psum.tile([P, BANK], F32, name="bank%d" % bank)
+            for a in (lead, 1 - lead):
+                nc.tensor.matmul_mx(
+                    out=sums[t][:],
+                    lhsT=w_codes[part, a, g, t].bitcast(FP8X4),
+                    lhsT_scale=w_scales[part, a, g, t],
+                    rhs=frames[h][:, a, :].bitcast(FP4X4),
+                    rhs_scale=planes[:, a * J + h * BANK : a * J + (h + 1) * BANK],
+                    start=(a == lead),
+                    stop=(a != lead),
+                )
+
+        def square(part, g, h, t, lo, width):
+            cols = slice(lo, lo + width)
+            column = PACK * g + t
+            nc.scalar.activation(out=squared[part, g, h][:, t, cols], in_=sums[t][:, cols], func=ACT.Square, scale=root[:, column : column + 1])
+
+        def unit(part, g, h, slot, lead, widths):
+            squared[part, g, h] = sbuf([P, PACK, BANK], F32, slot)
+            for t in range(PACK):
+                transform(part, g, h, t, PACK * h + t, lead)
+            lo = 0
+            for width in widths:
+                for t in range(PACK):
+                    square(part, g, h, t, lo, width)
+                lo += width
 
         def add_squares(g, h, lo, width, slot):
-            tile = keep.tile([P, PACK * width], BF16, name=slot, align_bytes=64)
+            tile = sbuf([P, PACK * width], BF16, slot)
             cols = slice(lo, lo + width)
             nc.vector.tensor_tensor(
-                out=tile[:, : PACK * width].rearrange("p (c i t) -> p c t i", i=2, t=PACK),
+                out=tile[:].rearrange("p (c i t) -> p c t i", i=2, t=PACK),
                 in0=squared["re", g, h][:, :, cols].rearrange("p t (c i) -> p c t i", i=2),
                 in1=squared["im", g, h][:, :, cols].rearrange("p t (c i) -> p c t i", i=2),
                 op=ALU.add,
@@ -167,17 +166,10 @@ def tile_list_meltab_pow_kernel(tc, tab_words, tab_scales, co, si, gn, fb, offs,
 
         def quantise_power(g, h, lo, width):
             cols = slice(h * BANK + lo, h * BANK + lo + width)
-            nc.vector.quantize_mx(out=h_codes[g][:, cols].bitcast(FP8X4), scales=h_scales[g][:, cols], in_=power[g, h, lo][:, : PACK * width])
+            nc.vector.quantize_mx(out=h_codes[g][:, cols].bitcast(FP8X4), scales=h_scales[g][:, cols], in_=power[g, h, lo][:])
 
-        fb_codes, fb_scales = {}, {}
-
-        def load_filters(g):
-            tile = keep.tile([P, PACK, N], F32, name="fb_raw%d" % g, align_bytes=64)
-            nc.sync.dma_start(out=tile[:], in_=fb[g * PASS : (g + 1) * PASS, :].rearrange("(p t) n -> p t n", t=PACK))
-            raw["fb", g] = tile
-
-        def cast_filters(g, slot):
-            tile = keep.tile([P, PACK * N], BF16, name=slot, align_bytes=64)
+        def cast_filters(g):
+            tile = sbuf([P, PACK * N], BF16, "grouped_fb%d" % g)
             nc.vector.tensor_tensor(
                 out=tile[:].rearrange("p (c i t) -> p c t i", i=2, t=PACK),
                 in0=raw["fb", g][:].rearrange("p t (c i) -> p c t i", i=2),
@@ -186,20 +178,20 @@ def tile_list_meltab_pow_kernel(tc, tab_words, tab_scales, co, si, gn, fb, offs,
             )
             grouped["fb", g] = tile
 
-        def quantise_filters(g, slot):
-            fb_codes[g] = keep.tile([P, N], U32, name=slot, align_bytes=64)
-            fb_scales[g] = keep.tile([P, N], U8, name="fb_scales%d" % g, align_bytes=64)
+        def quantise_filters(g):
+            fb_codes[g] = sbuf([P, N], U32, "fb_codes%d" % g)
+            fb_scales[g] = sbuf([P, N], U8, "fb_scales%d" % g)
             nc.vector.quantize_mx(out=fb_codes[g][:].bitcast(FP8X4), scales=fb_scales[g][:], in_=grouped["fb", g][:])
 
-        def filter_bank(lo, width, first, engine):
+        def filter_bank(lo, width, bank, engine):
             frames_cols = slice(lo, lo + width)
-            result = results.tile([P, 2, BANK], F32, name="result", align_bytes=64)
+            result = sbuf([P, 2, width], F32, "result%d" % lo)
+            total = psum.tile([P, 2, width], F32, name="bank%d" % bank)
             for b in range(2):
-                bank = psum.tile([P, BANK], F32, name="bank%d" % (first + b))
                 for g in range(2):
                     cols = slice(b * P, (b + 1) * P)
                     nc.tensor.matmul_mx(
-                        out=bank[:, :width],
+                        out=total[:, b, :],
                         lhsT=fb_codes[g][:, cols].bitcast(FP8X4),
                         lhsT_scale=fb_scales[g][:, cols],
                         rhs=h_codes[g][:, frames_cols].bitcast(FP8X4),
@@ -207,76 +199,104 @@ def tile_list_meltab_pow_kernel(tc, tab_words, tab_scales, co, si, gn, fb, offs,
                         start=(g == 0),
                         stop=(g == 1),
                     )
-                if engine == "scalar" or (engine == "both" and b == 0):
-                    nc.scalar.copy(out=result[:, b, :width], in_=bank[:, :width])
-                else:
-                    nc.vector.tensor_copy(out=result[:, b, :width], in_=bank[:, :width])
-            nc.sync.dma_start(out=out.rearrange("(b p) j -> p b j", p=P)[:, :, frames_cols], in_=result[:, :, :width])
+            if engine == "scalar":
+                nc.scalar.copy(out=result[:], in_=total[:])
+            else:
+                nc.vector.tensor_copy(out=result[:], in_=total[:])
+            nc.sync.dma_start(out=out.rearrange("(b p) j -> p b j", p=P)[:, :, frames_cols], in_=result[:])
 
-        load("re", 0, 0)
-        load_offsets()
+        nc.gpsimd.memset(scale_store[:, : T // 8], 0)
+        nc.vector.memset(scale_store[:, T // 8 :], 0)
+        nc.vector.memset(planes[:].bitcast(I32), 0)
+        load_table(0, T // 4)
+        nc.sync.dma_start(offsets[:], offs)
         load_scales()
         load_gain()
-        load_table()
-        load("re", 1, 0)
-        gather_scales()
+        load_table(T // 4, T)
+        load("re", 0, 0)
         prepare_gain()
+        gather_scales()
+        load("re", 1, 0)
         load("im", 0, 0)
-        cast("re", 0, 0, "scalar", "grpre00")
         load("im", 1, 0)
-        quantise_weight("re", 0, 0, "ss")
-        gather_words(0, "pw0")
-        part_words(0)
-        cast("re", 1, 0, "scalar", "grpre10")
-        load("re", 0, 1)
-        gather_words(1, "pw0")
-        quantise_weight("re", 1, 0, "wre10")
-        part_words(1)
-        transform("re", 0, 0, 0, 1, 0)
-        cast("im", 0, 0, "vector", "grpim00")
-        load("re", 1, 1)
-        cast("im", 1, 0, "vector", "grpim10")
         load_filters(0)
+        load("re", 0, 1)
+        load("re", 1, 1)
         load("im", 0, 1)
-        quantise_weight("im", 0, 0, "wim00")
-        quantise_weight("im", 1, 0, "wim10")
-        transform("re", 0, 1, 4, 1, 1)
-        transform("im", 0, 0, 0, 1, 0)
-        cast("re", 0, 1, "vector", "grpre01")
         load("im", 1, 1)
-        quantise_weight("re", 0, 1, "wre01")
-        cast("re", 1, 1, "vector", "grpre11")
         load_filters(1)
-        quantise_weight("re", 1, 1, "wre11")
-        cast_filters(0, "grpfb0")
-        transform("im", 0, 1, 4, 1, 1)
-        cast("im", 0, 1, "scalar", "grpim01")
-        add_squares(0, 0, 0, 512, "grpre11")
-        cast("im", 1, 1, "vector", "grpim11")
-        quantise_weight("im", 0, 1, "wim01")
-        quantise_weight("im", 1, 1, "wim11")
-        quantise_power(0, 0, 0, 512)
-        transform("re", 1, 0, 0, 1, 0)
-        transform("re", 1, 1, 4, 1, 1)
-        add_squares(0, 1, 0, 512, "grpim11")
-        cast_filters(1, "grpfb1")
-        quantise_power(0, 1, 0, 512)
-        quantise_filters(0, "wfb0")
-        quantise_filters(1, "wfb1")
-        transform("im", 1, 0, 0, 2, 0)
-        add_squares(1, 0, 0, 256, "pow10_0")
-        add_squares(1, 0, 256, 256, "pow10_256")
+        gather_words(0)
+        part_words(0, "frames0")
+        gather_words(1)
+        cast("re", 0, 0, 0, 1, "scalar")
+        cast("re", 0, 0, 1, 1, "scalar")
+        cast("re", 0, 0, 2, 2, "scalar")
+        cast("re", 1, 0, 2, 2, "scalar")
+        quantise_weight("re", 0, 0, 0, 1)
+        part_words(1, "grouped_re000")
+        quantise_weight("re", 0, 0, 1, 1)
+        cast("re", 1, 0, 0, 1, "vector")
+        cast("re", 1, 0, 1, 1, "vector")
+        quantise_weight("re", 1, 0, 0, 1)
+        quantise_weight("re", 1, 0, 1, 1)
+        quantise_weight("re", 0, 0, 2, 2, "grouped_re100")
+        quantise_weight("re", 1, 0, 2, 2)
+        first_slot = sbuf([P, 2, PACK, BANK], F32, "word_store")
+        squared["re", 0, 0], squared["re", 0, 1] = first_slot[:, 0], first_slot[:, 1]
+        for n, (h, t) in enumerate([(0, 0), (0, 1), (1, 0), (1, 1), (0, 2), (0, 3), (1, 2), (1, 3)]):
+            transform("re", 0, h, t, n, 0 if n < 3 else 1)
+            square("re", 0, h, t, 0, BANK)
+        for a in range(2):
+            cast("im", a, 0, 0, 2, "vector")
+            cast("im", a, 0, 2, 2, "vector")
+            quantise_weight("im", a, 0, 0, 2)
+            quantise_weight("im", a, 0, 2, 2)
+        unit("im", 0, 0, "raw_re00", 0, [BANK])
+        unit("im", 0, 1, "raw_re10", 1, [BANK])
+        cast_filters(0)
+        cast("re", 0, 1, 0, 2, "vector")
+        quantise_filters(0)
+        cast("re", 0, 1, 2, 2, "vector")
+        quantise_weight("re", 0, 1, 0, 2)
+        quantise_weight("re", 0, 1, 2, 2)
+        cast("re", 1, 1, 0, 2, "vector")
+        cast("re", 1, 1, 2, 2, "vector")
+        quantise_weight("re", 1, 1, 0, 2)
+        quantise_weight("re", 1, 1, 2, 2)
+        cast("im", 0, 1, 0, 2, "scalar")
+        cast("im", 0, 1, 2, 2, "scalar")
+        quantise_weight("im", 0, 1, 0, 2)
+        quantise_weight("im", 0, 1, 2, 2)
+        cast("im", 1, 1, 0, 2, "vector")
+        cast("im", 1, 1, 2, 2, "vector")
+        quantise_weight("im", 1, 1, 0, 2)
+        quantise_weight("im", 1, 1, 2, 2)
+        unit("re", 1, 0, "raw_im00", 0, [BANK])
+        add_squares(0, 0, 0, 256, "raw_re11")
+        add_squares(0, 0, 256, 256, "grouped_re110")
+        quantise_power(0, 0, 0, 256)
+        add_squares(0, 1, 0, 256, "grouped_re112")
+        quantise_power(0, 0, 256, 256)
+        add_squares(0, 1, 256, 256, "grouped_re110")
+        quantise_power(0, 1, 0, 256)
+        cast_filters(1)
+        quantise_power(0, 1, 256, 256)
+        quantise_filters(1)
+        unit("re", 1, 1, "raw_im10", 1, [BANK])
+        unit("im", 1, 0, "raw_re01", 0, [256, 256])
+        unit("im", 1, 1, "raw_re11", 1, [BANK])
+        add_squares(1, 0, 0, 256, "power_a")
+        add_squares(1, 0, 256, 256, "power_b")
         quantise_power(1, 0, 0, 256)
-        transform("im", 1, 1, 4, 2, 1)
         filter_bank(0, 256, 0, "scalar")
+        add_squares(1, 1, 0, 256, "power_c")
         quantise_power(1, 0, 256, 256)
-        add_squares(1, 1, 0, 256, "pow11_0")
-        filter_bank(256, 256, 2, "scalar")
+        filter_bank(256, 256, 1, "scalar")
+        add_squares(1, 1, 256, 128, "power_d")
         quantise_power(1, 1, 0, 256)
-        add_squares(1, 1, 256, 128, "pow11_256")
-        filter_bank(512, 256, 0, "scalar")
+        filter_bank(512, 256, 2, "scalar")
+        add_squares(1, 1, 384, 128, "power_e")
         quantise_power(1, 1, 256, 128)
-        add_squares(1, 1, 384, 128, "pow11_384")
-        filter_bank(768, 128, 2, "scalar")
+        filter_bank(768, 128, 3, "scalar")
         quantise_power(1, 1, 384, 128)
-        filter_bank(896, 128, 0, "both")
+        filter_bank(896, 128, 4, "vector")

@@ -187,8 +187,8 @@ def tile_list_meltab_pow_kernel(tc, tab_words, tab_scales, co, si, gn, fb, offs,
             frames_cols = slice(lo, lo + width)
             result = sbuf([P, 2, width], F32, "result%d" % lo)
             total = psum.tile([P, 2, width], F32, name="bank%d" % bank)
-            for b in range(2):
-                for g in range(2):
+            for g in range(2):
+                for b in range(2):
                     cols = slice(b * P, (b + 1) * P)
                     nc.tensor.matmul_mx(
                         out=total[:, b, :],
@@ -196,8 +196,8 @@ def tile_list_meltab_pow_kernel(tc, tab_words, tab_scales, co, si, gn, fb, offs,
                         lhsT_scale=fb_scales[g][:, cols],
                         rhs=h_codes[g][:, frames_cols].bitcast(FP8X4),
                         rhs_scale=h_scales[g][:, frames_cols],
-                        start=(g == 0),
-                        stop=(g == 1),
+                        start=(g == 0 and b == 0),
+                        stop=(g == 1 and b == 1),
                     )
             if engine == "scalar":
                 nc.scalar.copy(out=result[:], in_=total[:])
@@ -246,11 +246,16 @@ def tile_list_meltab_pow_kernel(tc, tab_words, tab_scales, co, si, gn, fb, offs,
         for n, (h, t) in enumerate([(0, 0), (0, 1), (1, 0), (1, 1), (0, 2), (0, 3), (1, 2), (1, 3)]):
             transform("re", 0, h, t, n, 0 if n < 3 else 1)
             square("re", 0, h, t, 0, BANK)
-        for a in range(2):
-            cast("im", a, 0, 0, 2, "vector")
-            cast("im", a, 0, 2, 2, "vector")
-            quantise_weight("im", a, 0, 0, 2)
-            quantise_weight("im", a, 0, 2, 2)
+        cast("im", 0, 0, 0, 2, "vector")
+        cast("im", 0, 0, 2, 2, "vector")
+        quantise_weight("im", 0, 0, 0, 2)
+        quantise_weight("im", 0, 0, 2, 2)
+        cast("im", 1, 0, 0, 2, "vector")
+        cast("im", 1, 0, 2, 1, "vector")
+        quantise_weight("im", 1, 0, 0, 2)
+        cast("im", 1, 0, 3, 1, "vector")
+        quantise_weight("im", 1, 0, 2, 1)
+        quantise_weight("im", 1, 0, 3, 1)
         unit("im", 0, 0, "raw_re00", 0, [BANK])
         unit("im", 0, 1, "raw_re10", 1, [BANK])
         cast_filters(0)
@@ -260,31 +265,34 @@ def tile_list_meltab_pow_kernel(tc, tab_words, tab_scales, co, si, gn, fb, offs,
         quantise_weight("re", 0, 1, 0, 2)
         quantise_weight("re", 0, 1, 2, 2)
         cast("re", 1, 1, 0, 2, "vector")
-        cast("re", 1, 1, 2, 2, "vector")
+        cast("re", 1, 1, 2, 2, "scalar")
         quantise_weight("re", 1, 1, 0, 2)
+        add_squares(0, 0, 0, 256, "grouped_re010")
+        quantise_power(0, 0, 0, 256)
+        add_squares(0, 0, 256, 256, "grouped_re012")
         quantise_weight("re", 1, 1, 2, 2)
         cast("im", 0, 1, 0, 2, "scalar")
-        cast("im", 0, 1, 2, 2, "scalar")
+        cast("im", 0, 1, 2, 2, "vector")
         quantise_weight("im", 0, 1, 0, 2)
         quantise_weight("im", 0, 1, 2, 2)
         cast("im", 1, 1, 0, 2, "vector")
         cast("im", 1, 1, 2, 2, "vector")
         quantise_weight("im", 1, 1, 0, 2)
         quantise_weight("im", 1, 1, 2, 2)
-        unit("re", 1, 0, "raw_im00", 0, [BANK])
-        add_squares(0, 0, 0, 256, "raw_re11")
-        add_squares(0, 0, 256, 256, "grouped_re110")
-        quantise_power(0, 0, 0, 256)
-        add_squares(0, 1, 0, 256, "grouped_re112")
+        squared["re", 1, 0] = sbuf([P, PACK, BANK], F32, "raw_im00")
+        squared["re", 1, 1] = sbuf([P, PACK, BANK], F32, "raw_im10")
+        for n, (h, t) in enumerate([(0, 0), (0, 1), (1, 0), (1, 1), (0, 2), (0, 3), (1, 2), (1, 3)]):
+            transform("re", 1, h, t, n, 0 if n < 4 else 1)
+            square("re", 1, h, t, 0, BANK)
+        add_squares(0, 1, 0, 256, "grouped_re110")
         quantise_power(0, 0, 256, 256)
-        add_squares(0, 1, 256, 256, "grouped_re110")
+        add_squares(0, 1, 256, 256, "grouped_re112")
         quantise_power(0, 1, 0, 256)
         cast_filters(1)
         quantise_power(0, 1, 256, 256)
         quantise_filters(1)
-        unit("re", 1, 1, "raw_im10", 1, [BANK])
         unit("im", 1, 0, "raw_re01", 0, [256, 256])
-        unit("im", 1, 1, "raw_re11", 1, [BANK])
+        unit("im", 1, 1, "raw_re11", 1, [256, 256])
         add_squares(1, 0, 0, 256, "power_a")
         add_squares(1, 0, 256, 256, "power_b")
         quantise_power(1, 0, 0, 256)

@@ -178,8 +178,8 @@ def tile_list_meltab_pow_kernel(tc, tab_words, tab_scales, co, si, gn, fb, offs,
             )
             grouped["fb", g] = tile
 
-        def quantise_filters(g):
-            fb_codes[g] = sbuf([P, N], U32, "fb_codes%d" % g)
+        def quantise_filters(g, slot=None):
+            fb_codes[g] = sbuf([P, N], U32, slot or "fb_codes%d" % g)
             fb_scales[g] = sbuf([P, N], U8, "fb_scales%d" % g)
             nc.vector.quantize_mx(out=fb_codes[g][:].bitcast(FP8X4), scales=fb_scales[g][:], in_=grouped["fb", g][:])
 
@@ -203,6 +203,26 @@ def tile_list_meltab_pow_kernel(tc, tab_words, tab_scales, co, si, gn, fb, offs,
                 nc.scalar.copy(out=result[:], in_=total[:])
             else:
                 nc.vector.tensor_copy(out=result[:], in_=total[:])
+            nc.sync.dma_start(out=out.rearrange("(b p) j -> p b j", p=P)[:, :, frames_cols], in_=result[:])
+
+        def filter_bank_split(lo, width, first_bank):
+            frames_cols = slice(lo, lo + width)
+            totals = [psum.tile([P, width], F32, name="bank%d" % (first_bank + b)) for b in range(2)]
+            for g in range(2):
+                for b in range(2):
+                    cols = slice(b * P, (b + 1) * P)
+                    nc.tensor.matmul_mx(
+                        out=totals[b][:],
+                        lhsT=fb_codes[g][:, cols].bitcast(FP8X4),
+                        lhsT_scale=fb_scales[g][:, cols],
+                        rhs=h_codes[g][:, frames_cols].bitcast(FP8X4),
+                        rhs_scale=h_scales[g][:, frames_cols],
+                        start=(g == 0),
+                        stop=(g == 1),
+                    )
+            result = sbuf([P, 2, width], F32, "result%d" % lo)
+            nc.vector.tensor_copy(out=result[:, 0, :], in_=totals[0][:])
+            nc.scalar.copy(out=result[:, 1, :], in_=totals[1][:])
             nc.sync.dma_start(out=out.rearrange("(b p) j -> p b j", p=P)[:, :, frames_cols], in_=result[:])
 
         nc.gpsimd.memset(scale_store[:, : T // 8], 0)
@@ -260,38 +280,40 @@ def tile_list_meltab_pow_kernel(tc, tab_words, tab_scales, co, si, gn, fb, offs,
         unit("im", 0, 1, "raw_re10", 1, [BANK])
         cast_filters(0)
         cast("re", 0, 1, 0, 2, "vector")
-        quantise_filters(0)
         cast("re", 0, 1, 2, 2, "vector")
         quantise_weight("re", 0, 1, 0, 2)
         quantise_weight("re", 0, 1, 2, 2)
-        cast("re", 1, 1, 0, 2, "vector")
+        quantise_filters(0, "raw_re01")
+        cast("re", 1, 1, 0, 1, "vector")
+        cast("re", 1, 1, 1, 1, "vector")
         cast("re", 1, 1, 2, 2, "scalar")
-        quantise_weight("re", 1, 1, 0, 2)
-        add_squares(0, 0, 0, 256, "grouped_re010")
+        quantise_weight("re", 1, 1, 0, 1)
+        quantise_weight("re", 1, 1, 1, 1)
+        add_squares(0, 0, 0, 256, "grouped_re110")
         quantise_power(0, 0, 0, 256)
-        add_squares(0, 0, 256, 256, "grouped_re012")
+        add_squares(0, 0, 256, 256, "grouped_re111")
         quantise_weight("re", 1, 1, 2, 2)
         cast("im", 0, 1, 0, 2, "scalar")
-        cast("im", 0, 1, 2, 2, "vector")
-        quantise_weight("im", 0, 1, 0, 2)
-        quantise_weight("im", 0, 1, 2, 2)
+        cast("im", 0, 1, 2, 2, "scalar")
         cast("im", 1, 1, 0, 2, "vector")
         cast("im", 1, 1, 2, 2, "vector")
         quantise_weight("im", 1, 1, 0, 2)
+        quantise_weight("im", 0, 1, 0, 2, "raw_im11")
         quantise_weight("im", 1, 1, 2, 2)
+        quantise_weight("im", 0, 1, 2, 2, "grouped_im110")
         squared["re", 1, 0] = sbuf([P, PACK, BANK], F32, "raw_im00")
         squared["re", 1, 1] = sbuf([P, PACK, BANK], F32, "raw_im10")
         for n, (h, t) in enumerate([(0, 0), (0, 1), (1, 0), (1, 1), (0, 2), (0, 3), (1, 2), (1, 3)]):
             transform("re", 1, h, t, n, 0 if n < 4 else 1)
             square("re", 1, h, t, 0, BANK)
-        add_squares(0, 1, 0, 256, "grouped_re110")
+        add_squares(0, 1, 0, 256, "grouped_re112")
         quantise_power(0, 0, 256, 256)
-        add_squares(0, 1, 256, 256, "grouped_re112")
+        add_squares(0, 1, 256, 256, "grouped_im112")
         quantise_power(0, 1, 0, 256)
         cast_filters(1)
         quantise_power(0, 1, 256, 256)
         quantise_filters(1)
-        unit("im", 1, 0, "raw_re01", 0, [256, 256])
+        unit("im", 1, 0, "late_squares", 1, [256, 256])
         unit("im", 1, 1, "raw_re11", 1, [256, 256])
         add_squares(1, 0, 0, 256, "power_a")
         add_squares(1, 0, 256, 256, "power_b")
@@ -307,4 +329,4 @@ def tile_list_meltab_pow_kernel(tc, tab_words, tab_scales, co, si, gn, fb, offs,
         quantise_power(1, 1, 256, 128)
         filter_bank(768, 128, 3, "scalar")
         quantise_power(1, 1, 384, 128)
-        filter_bank(896, 128, 4, "vector")
+        filter_bank_split(896, 128, 4)

@@ -20,7 +20,8 @@ P = 128
 PACK = 4
 PASS = P * PACK
 BANK = 512
-TINY = 2.0 ** -70
+WIDE = 256
+NARROW = 128
 
 
 def tile_list_meltab_pow_kernel(tc, tab_words, tab_scales, co, si, gn, fb, offs, out):
@@ -32,64 +33,44 @@ def tile_list_meltab_pow_kernel(tc, tab_words, tab_scales, co, si, gn, fb, offs,
         def sbuf(shape, dtype, slot):
             return keep.tile(shape, dtype, name=slot, align_bytes=64)
 
+        def copy(engine, dst, src):
+            if engine == "scalar":
+                nc.scalar.copy(out=dst, in_=src)
+            else:
+                nc.vector.tensor_copy(out=dst, in_=src)
+
         offsets = keep.tile([P, J // 16], U16, name="offsets")
         scale_store = sbuf([P, T // 4], I32, "scale_store")
         word_store = sbuf([P, T], I32, "word_store")
         picked_scales = sbuf([P, J], U8, "picked_scales")
-        planes = sbuf([P, 2 * J], U8, "planes")
+        frame_scales = sbuf([P, 2 * J], U8, "frame_scales")
         picked_words = [sbuf([P, BANK], U32, "picked_words%d" % h) for h in range(2)]
-        frames = {}
         gain = keep.tile([P, 2, 2 * PACK], F32, name="gain")
         root = keep.tile([P, 2 * PACK], F32, name="root")
         sign = keep.tile([P, 2, PACK], F32, name="sign")
-        weights = {"re": co, "im": si}
-        raw, grouped, w_codes, w_scales, squared, power = {}, {}, {}, {}, {}, {}
-        fb_codes, fb_scales = {}, {}
         h_codes = [sbuf([P, J], U32, "h_codes%d" % g) for g in range(2)]
         h_scales = [sbuf([P, J], U8, "h_scales%d" % g) for g in range(2)]
+        weights = {"re": co, "im": si}
+        raw, rounded, w_codes, w_scales = {}, {}, {}, {}
+        frames, sums, squared, power, fb_codes, fb_scales = {}, {}, {}, {}, {}, {}
 
-        def load_table(lo, hi):
+
+        def load_table(first, last):
             words = tab_words[0].rearrange("p t b -> p (t b)").bitcast(I32)
-            nc.sync.dma_start(out=word_store[:, lo:hi], in_=words[:, lo:hi])
+            nc.sync.dma_start(out=word_store[:, first:last], in_=words[:, first:last])
 
         def load_scales():
             rows = tab_scales.bitcast(I32).rearrange("a q t -> q a t")
             nc.sync.dma_start(out=scale_store[0:P:4, :], in_=rows)
 
-        def load_gain():
-            runs = gn.rearrange("(g q e) -> q g e", g=2, e=2 * PACK)
-            for r in range(2):
-                nc.sync.dma_start(out=gain[r:P:2, :, :7], in_=runs[:, :, r : r + 7])
-
-        def load(part, a, g):
-            tile = sbuf([P, PACK, BANK], F32, "raw_%s%d%d" % (part, a, g))
-            rows = weights[part][a * PASS : (a + 1) * PASS, g * BANK : (g + 1) * BANK]
-            nc.sync.dma_start(out=tile[:], in_=rows.rearrange("(p i) f -> p i f", i=PACK))
-            raw[part, a, g] = tile
-
-        def load_filters(g):
-            tile = sbuf([P, PACK, N], F32, "fb_raw%d" % g)
-            rows = fb[g * PASS : (g + 1) * PASS, :].rearrange("(q t r) n -> r q t n", t=PACK, r=2)
-            for r in range(2):
-                nc.sync.dma_start(out=tile[r:P:2], in_=rows[r])
-            raw["fb", g] = tile
-
-        def prepare_gain():
-            flat = gain[:].rearrange("p g (t r) -> p (g t) r", r=2)[:, :, 0]
-            flat_sign = sign[:].rearrange("p g t -> p (g t)")
-            twice = keep.tile([P, 2 * PACK], F32, name="twice")
-            size = keep.tile([P, 2 * PACK], F32, name="size")
-            half = keep.tile([P, 2 * PACK], F32, name="half")
-            nc.gpsimd.memset(half[:], 0.5)
-            nc.gpsimd.tensor_scalar(out=twice[:], in0=flat, scalar1=0.0, scalar2=2.0, op0=ALU.is_ge, op1=ALU.mult)
-            nc.gpsimd.tensor_scalar(out=flat_sign, in0=twice[:], scalar1=-1.0, scalar2=None, op0=ALU.add)
-            nc.gpsimd.tensor_tensor(out=size[:], in0=flat, in1=flat_sign, op=ALU.mult)
-            nc.gpsimd.tensor_tensor(out=root[:], in0=size[:], in1=half[:], op=ALU.pow)
-
         def gather_scales():
             nc.vector.tensor_copy(picked_scales[:], scale_store[:].bitcast(U8).indirect(offsets[:]))
-            for q in (0, 2, 1, 3):
-                nc.sync.dma_start(out=planes[32 * q : 32 * q + 4, :].bitcast(I32), in_=picked_scales[32 * q : 32 * (q + 1) : 4, :].bitcast(I32))
+            for quadrant in (0, 2, 1, 3):
+                first = 32 * quadrant
+                nc.sync.dma_start(
+                    out=frame_scales[first : first + 4, :].bitcast(I32),
+                    in_=picked_scales[first : first + 32 : 4, :].bitcast(I32),
+                )
 
         def gather_words(h):
             window = word_store[:].bitcast(U32)
@@ -102,28 +83,50 @@ def tile_list_meltab_pow_kernel(tc, tab_words, tab_scales, co, si, gn, fb, offs,
                 in_=picked_words[h][:].bitcast(U16).rearrange("p (j a) -> p a j", a=2),
             )
 
+
+        def load_gain():
+            runs = gn.rearrange("(g q e) -> q g e", g=2, e=2 * PACK)
+            for r in range(2):
+                nc.sync.dma_start(out=gain[r:P:2, :, :6], in_=runs[:, :, 2 * r : 2 * r + 6])
+
+        def prepare_gain():
+            own = gain[:].rearrange("p g (u e) -> p (g u) e", u=2)[:, :, :2]
+            twice = keep.tile([P, PACK, 2], F32, name="twice")
+            size = keep.tile([P, PACK, 2], F32, name="size")
+            half = keep.tile([P, 2 * PACK], F32, name="half")
+            pairs = sign[:].rearrange("p g (u s) -> p (g u) s", u=2)
+            nc.gpsimd.memset(half[:], 0.5)
+            nc.gpsimd.tensor_scalar(out=twice[:], in0=own, scalar1=0.0, scalar2=2.0, op0=ALU.is_ge, op1=ALU.mult)
+            nc.gpsimd.tensor_scalar(out=pairs, in0=twice[:], scalar1=-1.0, scalar2=None, op0=ALU.add)
+            nc.gpsimd.tensor_tensor(out=size[:], in0=own, in1=pairs, op=ALU.mult)
+            nc.gpsimd.tensor_tensor(out=root[:], in0=size[:].rearrange("p a s -> p (a s)"), in1=half[:], op=ALU.pow)
+
+
+        def load(part, a, g):
+            tile = sbuf([P, PACK, BANK], F32, "raw_%s%d%d" % (part, a, g))
+            rows = weights[part][a * PASS : (a + 1) * PASS, g * BANK : (g + 1) * BANK]
+            nc.sync.dma_start(out=tile[:], in_=rows.rearrange("(p i) f -> p i f", i=PACK))
+            raw[part, a, g] = tile
+
         def cast(part, a, g, first, count, engine):
-            tile = sbuf([P, count * BANK], BF16, "grouped_%s%d%d%d" % (part, a, g, first))
-            dst = tile[:].rearrange("p (t q r i) -> p t q i r", t=count, r=2, i=PACK)
-            src = raw[part, a, g][:].rearrange("p i (q t r) -> p t q i r", t=PACK, r=2)[:, first : first + count]
-            if engine == "scalar":
-                nc.scalar.copy(out=dst, in_=src)
-            else:
-                nc.vector.tensor_copy(out=dst, in_=src)
+            tile = sbuf([P, count * BANK], BF16, "rounded_%s%d%d%d" % (part, a, g, first))
+            u, s = divmod(first, 2)
+            dst = tile[:].rearrange("p (s q r i) -> p s q i r", s=count, r=2, i=PACK)
+            src = raw[part, a, g][:].rearrange("p i (q u r s) -> p u s q i r", u=2, r=2, s=2)
+            copy(engine, dst, src[:, u, s : s + count])
             for t in range(count):
-                grouped[part, a, g, first + t] = (tile, t)
+                rounded[part, a, g, first + t] = (tile, t)
 
         def quantise_weight(part, a, g, first, count, slot=None):
             name = "%s%d%d%d" % (part, a, g, first)
             codes = sbuf([P, count * P], U32, slot or "w_codes_" + name)
             scales = sbuf([P, count * P], U8, "w_scales_" + name)
-            tile, t = grouped[part, a, g, first]
-            nc.vector.quantize_mx(out=codes[:].bitcast(FP8X4), scales=scales[:], in_=tile[:, t * BANK : (t + count) * BANK])
+            tile, place = rounded[part, a, g, first]
+            nc.vector.quantize_mx(out=codes[:].bitcast(FP8X4), scales=scales[:], in_=tile[:, place * BANK : (place + count) * BANK])
             for t in range(count):
                 cols = slice(t * P, (t + 1) * P)
                 w_codes[part, a, g, first + t], w_scales[part, a, g, first + t] = codes[:, cols], scales[:, cols]
 
-        sums = {}
 
         def transform(part, g, h, t, bank, lead):
             sums[t] = psum.tile([P, BANK], F32, name="bank%d" % bank)
@@ -133,7 +136,7 @@ def tile_list_meltab_pow_kernel(tc, tab_words, tab_scales, co, si, gn, fb, offs,
                     lhsT=w_codes[part, a, g, t].bitcast(FP8X4),
                     lhsT_scale=w_scales[part, a, g, t],
                     rhs=frames[h][:, a, :].bitcast(FP4X4),
-                    rhs_scale=planes[:, a * J + h * BANK : a * J + (h + 1) * BANK],
+                    rhs_scale=frame_scales[:, a * J + h * BANK : a * J + (h + 1) * BANK],
                     start=(a == lead),
                     stop=(a != lead),
                 )
@@ -143,15 +146,19 @@ def tile_list_meltab_pow_kernel(tc, tab_words, tab_scales, co, si, gn, fb, offs,
             column = PACK * g + t
             nc.scalar.activation(out=squared[part, g, h][:, t, cols], in_=sums[t][:, cols], func=ACT.Square, scale=root[:, column : column + 1])
 
-        def unit(part, g, h, slot, lead, widths):
-            squared[part, g, h] = sbuf([P, PACK, BANK], F32, slot)
+        def squares_by_tile_pair(g, ahead):
+            order = [(h, t) for pair in range(2) for h in range(2) for t in (2 * pair, 2 * pair + 1)]
+            for bank, (h, t) in enumerate(order):
+                transform("re", g, h, t, bank, 0 if bank < ahead else 1)
+                square("re", g, h, t, 0, BANK)
+
+        def squares_by_half(g, h, slot, lead, width):
+            squared["im", g, h] = sbuf([P, PACK, BANK], F32, slot)
             for t in range(PACK):
-                transform(part, g, h, t, PACK * h + t, lead)
-            lo = 0
-            for width in widths:
+                transform("im", g, h, t, PACK * h + t, lead)
+            for lo in range(0, BANK, width):
                 for t in range(PACK):
-                    square(part, g, h, t, lo, width)
-                lo += width
+                    square("im", g, h, t, lo, width)
 
         def add_squares(g, h, lo, width, slot):
             tile = sbuf([P, PACK * width], BF16, slot)
@@ -168,66 +175,65 @@ def tile_list_meltab_pow_kernel(tc, tab_words, tab_scales, co, si, gn, fb, offs,
             cols = slice(h * BANK + lo, h * BANK + lo + width)
             nc.vector.quantize_mx(out=h_codes[g][:, cols].bitcast(FP8X4), scales=h_scales[g][:, cols], in_=power[g, h, lo][:])
 
+
+        def load_filters(g):
+            tile = sbuf([P, PACK, N], F32, "raw_fb%d" % g)
+            rows = fb[g * PASS : (g + 1) * PASS, :].rearrange("(q u r s) n -> u q r (s n)", u=2, r=2, s=2)
+            for u in range(2):
+                nc.sync.dma_start(out=tile[:, 2 * u : 2 * u + 2, :].rearrange("p s n -> p (s n)"), in_=rows[u])
+            raw["fb", g] = tile
+
         def cast_filters(g):
-            tile = sbuf([P, PACK * N], BF16, "grouped_fb%d" % g)
+            tile = sbuf([P, PACK * N], BF16, "rounded_fb%d" % g)
             nc.vector.tensor_tensor(
                 out=tile[:].rearrange("p (c i t) -> p c t i", i=2, t=PACK),
                 in0=raw["fb", g][:].rearrange("p t (c i) -> p c t i", i=2),
                 in1=sign[:, g, :].unsqueeze(1).unsqueeze(3).to_broadcast([P, N // 2, PACK, 2]),
                 op=ALU.mult,
             )
-            grouped["fb", g] = tile
+            rounded["fb", g] = tile
 
-        def quantise_filters(g, slot=None):
-            fb_codes[g] = sbuf([P, N], U32, slot or "fb_codes%d" % g)
+        def quantise_filters(g, slot):
+            fb_codes[g] = sbuf([P, N], U32, slot)
             fb_scales[g] = sbuf([P, N], U8, "fb_scales%d" % g)
-            nc.vector.quantize_mx(out=fb_codes[g][:].bitcast(FP8X4), scales=fb_scales[g][:], in_=grouped["fb", g][:])
+            nc.vector.quantize_mx(out=fb_codes[g][:].bitcast(FP8X4), scales=fb_scales[g][:], in_=rounded["fb", g][:])
 
-        def filter_bank(lo, width, bank, engine):
-            frames_cols = slice(lo, lo + width)
+        def filter_pass(total, g, b, cols, start, stop):
+            rows = slice(b * P, (b + 1) * P)
+            nc.tensor.matmul_mx(
+                out=total,
+                lhsT=fb_codes[g][:, rows].bitcast(FP8X4),
+                lhsT_scale=fb_scales[g][:, rows],
+                rhs=h_codes[g][:, cols].bitcast(FP8X4),
+                rhs_scale=h_scales[g][:, cols],
+                start=start,
+                stop=stop,
+            )
+
+        def filter_bank(lo, width, bank):
+            cols = slice(lo, lo + width)
             result = sbuf([P, 2, width], F32, "result%d" % lo)
             total = psum.tile([P, 2, width], F32, name="bank%d" % bank)
             for g in range(2):
                 for b in range(2):
-                    cols = slice(b * P, (b + 1) * P)
-                    nc.tensor.matmul_mx(
-                        out=total[:, b, :],
-                        lhsT=fb_codes[g][:, cols].bitcast(FP8X4),
-                        lhsT_scale=fb_scales[g][:, cols],
-                        rhs=h_codes[g][:, frames_cols].bitcast(FP8X4),
-                        rhs_scale=h_scales[g][:, frames_cols],
-                        start=(g == 0 and b == 0),
-                        stop=(g == 1 and b == 1),
-                    )
-            if engine == "scalar":
-                nc.scalar.copy(out=result[:], in_=total[:])
-            else:
-                nc.vector.tensor_copy(out=result[:], in_=total[:])
-            nc.sync.dma_start(out=out.rearrange("(b p) j -> p b j", p=P)[:, :, frames_cols], in_=result[:])
+                    filter_pass(total[:, b, :], g, b, cols, g == 0 and b == 0, g == 1 and b == 1)
+            copy("scalar", result[:], total[:])
+            nc.sync.dma_start(out=out.rearrange("(b p) j -> p b j", p=P)[:, :, cols], in_=result[:])
 
-        def filter_bank_split(lo, width, first_bank):
-            frames_cols = slice(lo, lo + width)
+        def last_filter_bank(lo, width, first_bank):
+            cols = slice(lo, lo + width)
             totals = [psum.tile([P, width], F32, name="bank%d" % (first_bank + b)) for b in range(2)]
             for g in range(2):
                 for b in range(2):
-                    cols = slice(b * P, (b + 1) * P)
-                    nc.tensor.matmul_mx(
-                        out=totals[b][:],
-                        lhsT=fb_codes[g][:, cols].bitcast(FP8X4),
-                        lhsT_scale=fb_scales[g][:, cols],
-                        rhs=h_codes[g][:, frames_cols].bitcast(FP8X4),
-                        rhs_scale=h_scales[g][:, frames_cols],
-                        start=(g == 0),
-                        stop=(g == 1),
-                    )
+                    filter_pass(totals[b][:], g, b, cols, g == 0, g == 1)
             result = sbuf([P, 2, width], F32, "result%d" % lo)
-            nc.vector.tensor_copy(out=result[:, 0, :], in_=totals[0][:])
-            nc.scalar.copy(out=result[:, 1, :], in_=totals[1][:])
-            nc.sync.dma_start(out=out.rearrange("(b p) j -> p b j", p=P)[:, :, frames_cols], in_=result[:])
+            copy("vector", result[:, 0, :], totals[0][:])
+            copy("scalar", result[:, 1, :], totals[1][:])
+            nc.sync.dma_start(out=out.rearrange("(b p) j -> p b j", p=P)[:, :, cols], in_=result[:])
 
         nc.gpsimd.memset(scale_store[:, : T // 8], 0)
         nc.vector.memset(scale_store[:, T // 8 :], 0)
-        nc.vector.memset(planes[:].bitcast(I32), 0)
+        nc.vector.memset(frame_scales[:].bitcast(I32), 0)
         load_table(0, T // 4)
         nc.sync.dma_start(offsets[:], offs)
         load_scales()
@@ -245,6 +251,7 @@ def tile_list_meltab_pow_kernel(tc, tab_words, tab_scales, co, si, gn, fb, offs,
         load("im", 0, 1)
         load("im", 1, 1)
         load_filters(1)
+
         gather_words(0)
         part_words(0, "frames0")
         gather_words(1)
@@ -253,19 +260,18 @@ def tile_list_meltab_pow_kernel(tc, tab_words, tab_scales, co, si, gn, fb, offs,
         cast("re", 0, 0, 2, 2, "scalar")
         cast("re", 1, 0, 2, 2, "scalar")
         quantise_weight("re", 0, 0, 0, 1)
-        part_words(1, "grouped_re000")
+        part_words(1, "rounded_re000")
         quantise_weight("re", 0, 0, 1, 1)
         cast("re", 1, 0, 0, 1, "vector")
         cast("re", 1, 0, 1, 1, "vector")
         quantise_weight("re", 1, 0, 0, 1)
         quantise_weight("re", 1, 0, 1, 1)
-        quantise_weight("re", 0, 0, 2, 2, "grouped_re100")
+        quantise_weight("re", 0, 0, 2, 2, "rounded_re100")
         quantise_weight("re", 1, 0, 2, 2)
-        first_slot = sbuf([P, 2, PACK, BANK], F32, "word_store")
-        squared["re", 0, 0], squared["re", 0, 1] = first_slot[:, 0], first_slot[:, 1]
-        for n, (h, t) in enumerate([(0, 0), (0, 1), (1, 0), (1, 1), (0, 2), (0, 3), (1, 2), (1, 3)]):
-            transform("re", 0, h, t, n, 0 if n < 3 else 1)
-            square("re", 0, h, t, 0, BANK)
+        both_halves = sbuf([P, 2, PACK, BANK], F32, "word_store")
+        squared["re", 0, 0], squared["re", 0, 1] = both_halves[:, 0], both_halves[:, 1]
+        squares_by_tile_pair(0, 3)
+
         cast("im", 0, 0, 0, 2, "vector")
         cast("im", 0, 0, 2, 2, "vector")
         quantise_weight("im", 0, 0, 0, 2)
@@ -276,8 +282,9 @@ def tile_list_meltab_pow_kernel(tc, tab_words, tab_scales, co, si, gn, fb, offs,
         cast("im", 1, 0, 3, 1, "vector")
         quantise_weight("im", 1, 0, 2, 1)
         quantise_weight("im", 1, 0, 3, 1)
-        unit("im", 0, 0, "raw_re00", 0, [BANK])
-        unit("im", 0, 1, "raw_re10", 1, [BANK])
+        squares_by_half(0, 0, "raw_re00", 0, BANK)
+        squares_by_half(0, 1, "raw_re10", 1, BANK)
+
         cast_filters(0)
         cast("re", 0, 1, 0, 2, "vector")
         cast("re", 0, 1, 2, 2, "vector")
@@ -289,10 +296,11 @@ def tile_list_meltab_pow_kernel(tc, tab_words, tab_scales, co, si, gn, fb, offs,
         cast("re", 1, 1, 2, 2, "scalar")
         quantise_weight("re", 1, 1, 0, 1)
         quantise_weight("re", 1, 1, 1, 1)
-        add_squares(0, 0, 0, 256, "grouped_re110")
-        quantise_power(0, 0, 0, 256)
-        add_squares(0, 0, 256, 256, "grouped_re111")
+        add_squares(0, 0, 0, WIDE, "rounded_re110")
+        quantise_power(0, 0, 0, WIDE)
+        add_squares(0, 0, WIDE, WIDE, "rounded_re111")
         quantise_weight("re", 1, 1, 2, 2)
+
         cast("im", 0, 1, 0, 2, "scalar")
         cast("im", 0, 1, 2, 2, "scalar")
         cast("im", 1, 1, 0, 2, "vector")
@@ -300,33 +308,32 @@ def tile_list_meltab_pow_kernel(tc, tab_words, tab_scales, co, si, gn, fb, offs,
         quantise_weight("im", 1, 1, 0, 2)
         quantise_weight("im", 0, 1, 0, 2, "raw_im11")
         quantise_weight("im", 1, 1, 2, 2)
-        quantise_weight("im", 0, 1, 2, 2, "grouped_im110")
+        quantise_weight("im", 0, 1, 2, 2, "rounded_im110")
         squared["re", 1, 0] = sbuf([P, PACK, BANK], F32, "raw_im00")
         squared["re", 1, 1] = sbuf([P, PACK, BANK], F32, "raw_im10")
-        for n, (h, t) in enumerate([(0, 0), (0, 1), (1, 0), (1, 1), (0, 2), (0, 3), (1, 2), (1, 3)]):
-            transform("re", 1, h, t, n, 0 if n < 4 else 1)
-            square("re", 1, h, t, 0, BANK)
-        add_squares(0, 1, 0, 256, "grouped_re112")
-        quantise_power(0, 0, 256, 256)
-        add_squares(0, 1, 256, 256, "grouped_im112")
-        quantise_power(0, 1, 0, 256)
+        squares_by_tile_pair(1, PACK)
+        add_squares(0, 1, 0, WIDE, "rounded_re112")
+        quantise_power(0, 0, WIDE, WIDE)
+        add_squares(0, 1, WIDE, WIDE, "rounded_im112")
+        quantise_power(0, 1, 0, WIDE)
         cast_filters(1)
-        quantise_power(0, 1, 256, 256)
-        quantise_filters(1)
-        unit("im", 1, 0, "late_squares", 1, [256, 256])
-        unit("im", 1, 1, "raw_re11", 1, [256, 256])
-        add_squares(1, 0, 0, 256, "power_a")
-        add_squares(1, 0, 256, 256, "power_b")
-        quantise_power(1, 0, 0, 256)
-        filter_bank(0, 256, 0, "scalar")
-        add_squares(1, 1, 0, 256, "power_c")
-        quantise_power(1, 0, 256, 256)
-        filter_bank(256, 256, 1, "scalar")
-        add_squares(1, 1, 256, 128, "power_d")
-        quantise_power(1, 1, 0, 256)
-        filter_bank(512, 256, 2, "scalar")
-        add_squares(1, 1, 384, 128, "power_e")
-        quantise_power(1, 1, 256, 128)
-        filter_bank(768, 128, 3, "scalar")
-        quantise_power(1, 1, 384, 128)
-        filter_bank_split(896, 128, 4)
+        quantise_power(0, 1, WIDE, WIDE)
+        quantise_filters(1, "fb_codes1")
+        squares_by_half(1, 0, "late_squares", 1, WIDE)
+        squares_by_half(1, 1, "raw_re11", 1, WIDE)
+
+        add_squares(1, 0, 0, WIDE, "power0")
+        add_squares(1, 0, WIDE, WIDE, "power1")
+        quantise_power(1, 0, 0, WIDE)
+        filter_bank(0, WIDE, 0)
+        add_squares(1, 1, 0, WIDE, "power2")
+        quantise_power(1, 0, WIDE, WIDE)
+        filter_bank(WIDE, WIDE, 1)
+        quantise_power(1, 1, 0, WIDE)
+        filter_bank(BANK, WIDE, 2)
+        add_squares(1, 1, WIDE, NARROW, "power3")
+        add_squares(1, 1, WIDE + NARROW, NARROW, "power4")
+        quantise_power(1, 1, WIDE, NARROW)
+        filter_bank(BANK + WIDE, NARROW, 3)
+        quantise_power(1, 1, WIDE + NARROW, NARROW)
+        last_filter_bank(J - NARROW, NARROW, 4)

@@ -60,7 +60,7 @@ def tile_list_meltab_pow_kernel(tc, tab_words, tab_scales, co, si, gn, fb, offs,
             nc.sync.dma_start(out=word_store[:, first:last], in_=words[:, first:last])
 
         def load_scales():
-            rows = tab_scales.bitcast(I32).rearrange("a q t -> q a t")
+            rows = tab_scales.bitcast(I32).rearrange("a m t -> m a t")
             nc.sync.dma_start(out=scale_store[0:P:4, :], in_=rows)
 
         def gather_scales():
@@ -99,7 +99,7 @@ def tile_list_meltab_pow_kernel(tc, tab_words, tab_scales, co, si, gn, fb, offs,
             nc.gpsimd.tensor_scalar(out=twice[:], in0=own, scalar1=0.0, scalar2=2.0, op0=ALU.is_ge, op1=ALU.mult)
             nc.gpsimd.tensor_scalar(out=pairs, in0=twice[:], scalar1=-1.0, scalar2=None, op0=ALU.add)
             nc.gpsimd.tensor_tensor(out=size[:], in0=own, in1=pairs, op=ALU.mult)
-            nc.gpsimd.tensor_tensor(out=root[:], in0=size[:].rearrange("p a s -> p (a s)"), in1=half[:], op=ALU.pow)
+            nc.gpsimd.tensor_tensor(out=root[:], in0=size[:].rearrange("p x s -> p (x s)"), in1=half[:], op=ALU.pow)
 
 
         def load(part, a, g):
@@ -146,10 +146,10 @@ def tile_list_meltab_pow_kernel(tc, tab_words, tab_scales, co, si, gn, fb, offs,
             column = PACK * g + t
             nc.scalar.activation(out=squared[part, g, h][:, t, cols], in_=sums[t][:, cols], func=ACT.Square, scale=root[:, column : column + 1])
 
-        def squares_by_tile_pair(g, ahead):
+        def squares_by_tile_pair(g):
             order = [(h, t) for pair in range(2) for h in range(2) for t in (2 * pair, 2 * pair + 1)]
             for bank, (h, t) in enumerate(order):
-                transform("re", g, h, t, bank, 0 if bank < ahead else 1)
+                transform("re", g, h, t, bank, 0 if t < 2 else 1)
                 square("re", g, h, t, 0, BANK)
 
         def squares_by_half(g, h, slot, lead, width):
@@ -164,9 +164,9 @@ def tile_list_meltab_pow_kernel(tc, tab_words, tab_scales, co, si, gn, fb, offs,
             tile = sbuf([P, PACK * width], BF16, slot)
             cols = slice(lo, lo + width)
             nc.vector.tensor_tensor(
-                out=tile[:].rearrange("p (c i t) -> p c t i", i=2, t=PACK),
-                in0=squared["re", g, h][:, :, cols].rearrange("p t (c i) -> p c t i", i=2),
-                in1=squared["im", g, h][:, :, cols].rearrange("p t (c i) -> p c t i", i=2),
+                out=tile[:].rearrange("p (c i t) -> p c t i", i=4, t=PACK),
+                in0=squared["re", g, h][:, :, cols].rearrange("p t (c i) -> p c t i", i=4),
+                in1=squared["im", g, h][:, :, cols].rearrange("p t (c i) -> p c t i", i=4),
                 op=ALU.add,
             )
             power[g, h, lo] = tile
@@ -186,9 +186,9 @@ def tile_list_meltab_pow_kernel(tc, tab_words, tab_scales, co, si, gn, fb, offs,
         def cast_filters(g):
             tile = sbuf([P, PACK * N], BF16, "rounded_fb%d" % g)
             nc.vector.tensor_tensor(
-                out=tile[:].rearrange("p (c i t) -> p c t i", i=2, t=PACK),
-                in0=raw["fb", g][:].rearrange("p t (c i) -> p c t i", i=2),
-                in1=sign[:, g, :].unsqueeze(1).unsqueeze(3).to_broadcast([P, N // 2, PACK, 2]),
+                out=tile[:].rearrange("p (c i t) -> p c t i", i=4, t=PACK),
+                in0=raw["fb", g][:].rearrange("p t (c i) -> p c t i", i=4),
+                in1=sign[:, g, :].unsqueeze(1).unsqueeze(3).to_broadcast([P, N // 4, PACK, 4]),
                 op=ALU.mult,
             )
             rounded["fb", g] = tile
@@ -220,7 +220,7 @@ def tile_list_meltab_pow_kernel(tc, tab_words, tab_scales, co, si, gn, fb, offs,
             copy("scalar", result[:], total[:])
             nc.sync.dma_start(out=out.rearrange("(b p) j -> p b j", p=P)[:, :, cols], in_=result[:])
 
-        def last_filter_bank(lo, width, first_bank):
+        def split_filter_bank(lo, width, first_bank):
             cols = slice(lo, lo + width)
             totals = [psum.tile([P, width], F32, name="bank%d" % (first_bank + b)) for b in range(2)]
             for g in range(2):
@@ -270,7 +270,7 @@ def tile_list_meltab_pow_kernel(tc, tab_words, tab_scales, co, si, gn, fb, offs,
         quantise_weight("re", 1, 0, 2, 2)
         both_halves = sbuf([P, 2, PACK, BANK], F32, "word_store")
         squared["re", 0, 0], squared["re", 0, 1] = both_halves[:, 0], both_halves[:, 1]
-        squares_by_tile_pair(0, 3)
+        squares_by_tile_pair(0)
 
         cast("im", 0, 0, 0, 2, "vector")
         cast("im", 0, 0, 2, 2, "vector")
@@ -311,7 +311,7 @@ def tile_list_meltab_pow_kernel(tc, tab_words, tab_scales, co, si, gn, fb, offs,
         quantise_weight("im", 0, 1, 2, 2, "rounded_im110")
         squared["re", 1, 0] = sbuf([P, PACK, BANK], F32, "raw_im00")
         squared["re", 1, 1] = sbuf([P, PACK, BANK], F32, "raw_im10")
-        squares_by_tile_pair(1, PACK)
+        squares_by_tile_pair(1)
         add_squares(0, 1, 0, WIDE, "rounded_re112")
         quantise_power(0, 0, WIDE, WIDE)
         add_squares(0, 1, WIDE, WIDE, "rounded_im112")
@@ -334,6 +334,6 @@ def tile_list_meltab_pow_kernel(tc, tab_words, tab_scales, co, si, gn, fb, offs,
         add_squares(1, 1, WIDE, NARROW, "power3")
         add_squares(1, 1, WIDE + NARROW, NARROW, "power4")
         quantise_power(1, 1, WIDE, NARROW)
-        filter_bank(BANK + WIDE, NARROW, 3)
+        split_filter_bank(BANK + WIDE, NARROW, 3)
         quantise_power(1, 1, WIDE + NARROW, NARROW)
-        last_filter_bank(J - NARROW, NARROW, 4)
+        split_filter_bank(J - NARROW, NARROW, 5)

@@ -111,9 +111,9 @@ def tile_list_meltab_pow_kernel(tc, tab_words, tab_scales, co, si, gn, fb, offs,
         def cast(part, a, g, first, count, engine):
             tile = sbuf([P, count * BANK], BF16, "rounded_%s%d%d%d" % (part, a, g, first))
             u, s = divmod(first, 2)
-            dst = tile[:].rearrange("p (s q r i) -> p s q i r", s=count, r=2, i=PACK)
-            src = raw[part, a, g][:].rearrange("p i (q u r s) -> p u s q i r", u=2, r=2, s=2)
-            copy(engine, dst, src[:, u, s : s + count])
+            dst = tile[:].rearrange("p (s q r i) -> p q i r s", s=count, r=2, i=PACK)
+            src = raw[part, a, g][:].rearrange("p i (q u r s) -> p u q i r s", u=2, r=2, s=2)
+            copy(engine, dst, src[:, u, :, :, :, s : s + count])
             for t in range(count):
                 rounded[part, a, g, first + t] = (tile, t)
 

@@ -152,13 +152,15 @@ def tile_list_meltab_pow_kernel(tc, tab_words, tab_scales, co, si, gn, fb, offs,
                 transform("re", g, h, t, bank, 0 if t < 2 else 1)
                 square("re", g, h, t, 0, BANK)
 
-        def squares_by_half(g, h, slot, lead, width):
-            squared["im", g, h] = sbuf([P, PACK, BANK], F32, slot)
+        def squares_by_half(part, g, h, slot, lead, widths):
+            squared[part, g, h] = sbuf([P, PACK, BANK], F32, slot)
             for t in range(PACK):
-                transform("im", g, h, t, PACK * h + t, lead)
-            for lo in range(0, BANK, width):
+                transform(part, g, h, t, PACK * h + t, lead)
+            lo = 0
+            for width in widths:
                 for t in range(PACK):
-                    square("im", g, h, t, lo, width)
+                    square(part, g, h, t, lo, width)
+                lo = lo + width
 
         def add_squares(g, h, lo, width, slot):
             tile = sbuf([P, PACK * width], BF16, slot)
@@ -272,56 +274,44 @@ def tile_list_meltab_pow_kernel(tc, tab_words, tab_scales, co, si, gn, fb, offs,
         squared["re", 0, 0], squared["re", 0, 1] = both_halves[:, 0], both_halves[:, 1]
         squares_by_tile_pair(0)
 
-        cast("im", 0, 0, 0, 2, "vector")
-        cast("im", 0, 0, 2, 2, "vector")
-        quantise_weight("im", 0, 0, 0, 2)
-        quantise_weight("im", 0, 0, 2, 2)
-        cast("im", 1, 0, 0, 2, "vector")
-        cast("im", 1, 0, 2, 1, "vector")
-        quantise_weight("im", 1, 0, 0, 2)
-        cast("im", 1, 0, 3, 1, "vector")
-        quantise_weight("im", 1, 0, 2, 1)
-        quantise_weight("im", 1, 0, 3, 1)
-        squares_by_half(0, 0, "raw_re00", 0, BANK)
-        squares_by_half(0, 1, "raw_re10", 1, BANK)
+        def vector_piece(part, a, g):
+            cast(part, a, g, 0, 2, "vector")
+            cast(part, a, g, 2, 2, "vector")
+            quantise_weight(part, a, g, 0, 2)
+            quantise_weight(part, a, g, 2, 2)
 
-        cast_filters(0)
-        cast("re", 0, 1, 0, 2, "vector")
-        cast("re", 0, 1, 2, 2, "vector")
-        quantise_weight("re", 0, 1, 0, 2)
-        quantise_weight("re", 0, 1, 2, 2)
-        quantise_filters(0, "raw_re01")
-        cast("re", 1, 1, 0, 1, "vector")
-        cast("re", 1, 1, 1, 1, "vector")
-        cast("re", 1, 1, 2, 2, "scalar")
-        quantise_weight("re", 1, 1, 0, 1)
-        quantise_weight("re", 1, 1, 1, 1)
-        add_squares(0, 0, 0, WIDE, "rounded_re110")
+        def shared_piece(part, a, g):
+            cast(part, a, g, 0, 2, "vector")
+            cast(part, a, g, 2, 2, "scalar")
+            quantise_weight(part, a, g, 0, 2)
+            quantise_weight(part, a, g, 2, 2)
+
+        vector_piece("im", 0, 0)
+        vector_piece("im", 1, 0)
+        shared_piece("re", 0, 1)
+        shared_piece("re", 1, 1)
+        vector_piece("im", 0, 1)
+        shared_piece("im", 1, 1)
+
+        squares_by_half("im", 0, 0, "raw_re00", 0, [WIDE, WIDE])
+        squares_by_half("im", 0, 1, "raw_re10", 1, [BANK])
+        add_squares(0, 0, 0, WIDE, "power00")
         quantise_power(0, 0, 0, WIDE)
-        add_squares(0, 0, WIDE, WIDE, "rounded_re111")
-        quantise_weight("re", 1, 1, 2, 2)
-
-        cast("im", 0, 1, 0, 2, "scalar")
-        cast("im", 0, 1, 2, 2, "scalar")
-        cast("im", 1, 1, 0, 2, "vector")
-        cast("im", 1, 1, 2, 2, "vector")
-        quantise_weight("im", 1, 1, 0, 2)
-        quantise_weight("im", 0, 1, 0, 2, "raw_im11")
-        quantise_weight("im", 1, 1, 2, 2)
-        quantise_weight("im", 0, 1, 2, 2, "rounded_im110")
-        squared["re", 1, 0] = sbuf([P, PACK, BANK], F32, "raw_im00")
-        squared["re", 1, 1] = sbuf([P, PACK, BANK], F32, "raw_im10")
-        squares_by_tile_pair(1)
-        add_squares(0, 1, 0, WIDE, "rounded_re112")
+        add_squares(0, 0, WIDE, WIDE, "power01")
         quantise_power(0, 0, WIDE, WIDE)
-        add_squares(0, 1, WIDE, WIDE, "rounded_im112")
+        add_squares(0, 1, 0, WIDE, "power02")
         quantise_power(0, 1, 0, WIDE)
-        cast_filters(1)
+        add_squares(0, 1, WIDE, WIDE, "power03")
         quantise_power(0, 1, WIDE, WIDE)
+        cast_filters(0)
+        quantise_filters(0, "fb_codes0")
+        cast_filters(1)
         quantise_filters(1, "fb_codes1")
-        squares_by_half(1, 0, "late_squares", 1, WIDE)
-        squares_by_half(1, 1, "raw_re11", 1, WIDE)
 
+        squares_by_half("re", 1, 0, "raw_im00", 0, [BANK])
+        squares_by_half("im", 1, 0, "late_squares", 0, [WIDE, WIDE])
+        squares_by_half("re", 1, 1, "raw_im10", 1, [BANK])
+        squares_by_half("im", 1, 1, "raw_re01", 1, [WIDE, WIDE])
         add_squares(1, 0, 0, WIDE, "power0")
         add_squares(1, 0, WIDE, WIDE, "power1")
         quantise_power(1, 0, 0, WIDE)

@@ -21,6 +21,7 @@ PACK = 4
 PASS = P * PACK
 BANK = 512
 WIDE = 256
+FIRST = 3 * T // 8
 NARROW = 128
 
 
@@ -233,14 +234,13 @@ def tile_list_meltab_pow_kernel(tc, tab_words, tab_scales, co, si, gn, fb, offs,
             copy("scalar", result[:, 1, :], totals[1][:])
             nc.sync.dma_start(out=out.rearrange("(b p) j -> p b j", p=P)[:, :, cols], in_=result[:])
 
-        nc.gpsimd.memset(scale_store[:, : T // 8], 0)
-        nc.vector.memset(scale_store[:, T // 8 :], 0)
+        nc.vector.memset(scale_store[:], 0)
         nc.vector.memset(frame_scales[:].bitcast(I32), 0)
-        load_table(0, T // 4)
+        load_table(0, FIRST)
         nc.sync.dma_start(offsets[:], offs)
         load_scales()
         load_gain()
-        load_table(T // 4, T)
+        load_table(FIRST, T)
         load("re", 0, 0)
         prepare_gain()
         gather_scales()
@@ -313,17 +313,15 @@ def tile_list_meltab_pow_kernel(tc, tab_words, tab_scales, co, si, gn, fb, offs,
         squares_by_half("re", 1, 1, "raw_im10", 1, [BANK])
         squares_by_half("im", 1, 1, "raw_re01", 1, [WIDE, WIDE])
         add_squares(1, 0, 0, WIDE, "power0")
-        add_squares(1, 0, WIDE, WIDE, "power1")
         quantise_power(1, 0, 0, WIDE)
         filter_bank(0, WIDE, 0)
-        add_squares(1, 1, 0, WIDE, "power2")
+        add_squares(1, 0, WIDE, WIDE, "power1")
         quantise_power(1, 0, WIDE, WIDE)
         filter_bank(WIDE, WIDE, 1)
-        quantise_power(1, 1, 0, WIDE)
-        filter_bank(BANK, WIDE, 2)
-        add_squares(1, 1, WIDE, NARROW, "power3")
-        add_squares(1, 1, WIDE + NARROW, NARROW, "power4")
-        quantise_power(1, 1, WIDE, NARROW)
-        split_filter_bank(BANK + WIDE, NARROW, 3)
-        quantise_power(1, 1, WIDE + NARROW, NARROW)
-        split_filter_bank(J - NARROW, NARROW, 5)
+        for lo in range(0, BANK, NARROW):
+            add_squares(1, 1, lo, NARROW, "power2%d" % lo)
+            quantise_power(1, 1, lo, NARROW)
+            if lo < WIDE:
+                filter_bank(BANK + lo, NARROW, 2 + lo // NARROW)
+            else:
+                split_filter_bank(BANK + lo, NARROW, 2 * (lo // NARROW))

@@ -247,11 +247,11 @@ def tile_list_meltab_pow_kernel(tc, tab_words, tab_scales, co, si, gn, fb, offs,
         load("re", 1, 0)
         load("im", 0, 0)
         load("im", 1, 0)
-        load_filters(0)
         load("re", 0, 1)
         load("re", 1, 1)
         load("im", 0, 1)
         load("im", 1, 1)
+        load_filters(0)
         load_filters(1)
 
         gather_words(0)
@@ -284,13 +284,12 @@ def tile_list_meltab_pow_kernel(tc, tab_words, tab_scales, co, si, gn, fb, offs,
             cast(part, a, g, 0, 2, "vector")
             cast(part, a, g, 2, 2, "scalar")
             quantise_weight(part, a, g, 0, 2)
-            quantise_weight(part, a, g, 2, 2)
 
         vector_piece("im", 0, 0)
         vector_piece("im", 1, 0)
-        shared_piece("re", 0, 1)
+        vector_piece("re", 0, 1)
         shared_piece("re", 1, 1)
-        vector_piece("im", 0, 1)
+        shared_piece("im", 0, 1)
         shared_piece("im", 1, 1)
 
         squares_by_half("im", 0, 0, "raw_re00", 0, [WIDE, WIDE])
@@ -298,10 +297,13 @@ def tile_list_meltab_pow_kernel(tc, tab_words, tab_scales, co, si, gn, fb, offs,
         add_squares(0, 0, 0, WIDE, "power00")
         quantise_power(0, 0, 0, WIDE)
         add_squares(0, 0, WIDE, WIDE, "power01")
+        quantise_weight("re", 1, 1, 2, 2)
         quantise_power(0, 0, WIDE, WIDE)
         add_squares(0, 1, 0, WIDE, "power02")
+        quantise_weight("im", 0, 1, 2, 2)
         quantise_power(0, 1, 0, WIDE)
         add_squares(0, 1, WIDE, WIDE, "power03")
+        quantise_weight("im", 1, 1, 2, 2)
         quantise_power(0, 1, WIDE, WIDE)
         cast_filters(0)
         quantise_filters(0, "fb_codes0")
@@ -309,8 +311,8 @@ def tile_list_meltab_pow_kernel(tc, tab_words, tab_scales, co, si, gn, fb, offs,
         quantise_filters(1, "fb_codes1")
 
         squares_by_half("re", 1, 0, "raw_im00", 0, [BANK])
-        squares_by_half("im", 1, 0, "late_squares", 0, [WIDE, WIDE])
         squares_by_half("re", 1, 1, "raw_im10", 1, [BANK])
+        squares_by_half("im", 1, 0, "late_squares", 0, [WIDE, WIDE])
         squares_by_half("im", 1, 1, "raw_re01", 1, [WIDE, WIDE])
         add_squares(1, 0, 0, WIDE, "power0")
         quantise_power(1, 0, 0, WIDE)

@@ -21,8 +21,8 @@ PACK = 4
 PASS = P * PACK
 BANK = 512
 WIDE = 256
-FIRST = 3 * T // 8
 NARROW = 128
+FIRST = 3 * T // 8
 
 
 def tile_list_meltab_pow_kernel(tc, tab_words, tab_scales, co, si, gn, fb, offs, out):
@@ -128,6 +128,17 @@ def tile_list_meltab_pow_kernel(tc, tab_words, tab_scales, co, si, gn, fb, offs,
                 cols = slice(t * P, (t + 1) * P)
                 w_codes[part, a, g, first + t], w_scales[part, a, g, first + t] = codes[:, cols], scales[:, cols]
 
+        def vector_piece(part, a, g):
+            cast(part, a, g, 0, 2, "vector")
+            cast(part, a, g, 2, 2, "vector")
+            quantise_weight(part, a, g, 0, 2)
+            quantise_weight(part, a, g, 2, 2)
+
+        def shared_piece(part, a, g):
+            cast(part, a, g, 0, 2, "vector")
+            cast(part, a, g, 2, 2, "scalar")
+            quantise_weight(part, a, g, 0, 2)
+
 
         def transform(part, g, h, t, bank, lead):
             sums[t] = psum.tile([P, BANK], F32, name="bank%d" % bank)
@@ -147,24 +158,24 @@ def tile_list_meltab_pow_kernel(tc, tab_words, tab_scales, co, si, gn, fb, offs,
             column = PACK * g + t
             nc.scalar.activation(out=squared[part, g, h][:, t, cols], in_=sums[t][:, cols], func=ACT.Square, scale=root[:, column : column + 1])
 
-        def squares_by_tile_pair(g):
+        def first_squares():
+            both_halves = sbuf([P, 2, PACK, BANK], F32, "word_store")
+            squared["re", 0, 0], squared["re", 0, 1] = both_halves[:, 0], both_halves[:, 1]
             order = [(h, t) for pair in range(2) for h in range(2) for t in (2 * pair, 2 * pair + 1)]
             for bank, (h, t) in enumerate(order):
-                transform("re", g, h, t, bank, 0 if t < 2 else 1)
-                square("re", g, h, t, 0, BANK)
+                transform("re", 0, h, t, bank, 0 if t < 2 else 1)
+                square("re", 0, h, t, 0, BANK)
 
-        def squares_by_half(part, g, h, slot, lead, widths):
+        def squares_by_half(part, g, h, slot, width):
             squared[part, g, h] = sbuf([P, PACK, BANK], F32, slot)
             for t in range(PACK):
-                transform(part, g, h, t, PACK * h + t, lead)
-            lo = 0
-            for width in widths:
+                transform(part, g, h, t, PACK * h + t, h)
+            for lo in range(0, BANK, width):
                 for t in range(PACK):
                     square(part, g, h, t, lo, width)
-                lo = lo + width
 
-        def add_squares(g, h, lo, width, slot):
-            tile = sbuf([P, PACK * width], BF16, slot)
+        def add_squares(g, h, lo, width):
+            tile = sbuf([P, PACK * width], BF16, "power%d%d_%d" % (g, h, lo))
             cols = slice(lo, lo + width)
             nc.vector.tensor_tensor(
                 out=tile[:].rearrange("p (c i t) -> p c t i", i=4, t=PACK),
@@ -196,8 +207,8 @@ def tile_list_meltab_pow_kernel(tc, tab_words, tab_scales, co, si, gn, fb, offs,
             )
             rounded["fb", g] = tile
 
-        def quantise_filters(g, slot):
-            fb_codes[g] = sbuf([P, N], U32, slot)
+        def quantise_filters(g):
+            fb_codes[g] = sbuf([P, N], U32, "fb_codes%d" % g)
             fb_scales[g] = sbuf([P, N], U8, "fb_scales%d" % g)
             nc.vector.quantize_mx(out=fb_codes[g][:].bitcast(FP8X4), scales=fb_scales[g][:], in_=rounded["fb", g][:])
 
@@ -231,8 +242,9 @@ def tile_list_meltab_pow_kernel(tc, tab_words, tab_scales, co, si, gn, fb, offs,
                     filter_pass(totals[b][:], g, b, cols, g == 0, g == 1)
             result = sbuf([P, 2, width], F32, "result%d" % lo)
             copy("vector", result[:, 0, :], totals[0][:])
+            nc.sync.dma_start(out=out[:P, cols], in_=result[:, 0, :])
             copy("scalar", result[:, 1, :], totals[1][:])
-            nc.sync.dma_start(out=out.rearrange("(b p) j -> p b j", p=P)[:, :, cols], in_=result[:])
+            nc.scalar.dma_start(out=out[P:, cols], in_=result[:, 1, :])
 
         nc.vector.memset(scale_store[:], 0)
         nc.vector.memset(frame_scales[:].bitcast(I32), 0)
@@ -270,60 +282,39 @@ def tile_list_meltab_pow_kernel(tc, tab_words, tab_scales, co, si, gn, fb, offs,
         quantise_weight("re", 1, 0, 1, 1)
         quantise_weight("re", 0, 0, 2, 2, "rounded_re100")
         quantise_weight("re", 1, 0, 2, 2)
-        both_halves = sbuf([P, 2, PACK, BANK], F32, "word_store")
-        squared["re", 0, 0], squared["re", 0, 1] = both_halves[:, 0], both_halves[:, 1]
-        squares_by_tile_pair(0)
+        first_squares()
 
-        def vector_piece(part, a, g):
-            cast(part, a, g, 0, 2, "vector")
-            cast(part, a, g, 2, 2, "vector")
-            quantise_weight(part, a, g, 0, 2)
-            quantise_weight(part, a, g, 2, 2)
-
-        def shared_piece(part, a, g):
-            cast(part, a, g, 0, 2, "vector")
-            cast(part, a, g, 2, 2, "scalar")
-            quantise_weight(part, a, g, 0, 2)
-
+        shared = [("re", 1, 1), ("im", 0, 1), ("im", 1, 1)]
         vector_piece("im", 0, 0)
         vector_piece("im", 1, 0)
         vector_piece("re", 0, 1)
-        shared_piece("re", 1, 1)
-        shared_piece("im", 0, 1)
-        shared_piece("im", 1, 1)
+        for piece in shared:
+            shared_piece(*piece)
 
-        squares_by_half("im", 0, 0, "raw_re00", 0, [WIDE, WIDE])
-        squares_by_half("im", 0, 1, "raw_re10", 1, [BANK])
-        add_squares(0, 0, 0, WIDE, "power00")
-        quantise_power(0, 0, 0, WIDE)
-        add_squares(0, 0, WIDE, WIDE, "power01")
-        quantise_weight("re", 1, 1, 2, 2)
-        quantise_power(0, 0, WIDE, WIDE)
-        add_squares(0, 1, 0, WIDE, "power02")
-        quantise_weight("im", 0, 1, 2, 2)
-        quantise_power(0, 1, 0, WIDE)
-        add_squares(0, 1, WIDE, WIDE, "power03")
-        quantise_weight("im", 1, 1, 2, 2)
-        quantise_power(0, 1, WIDE, WIDE)
-        cast_filters(0)
-        quantise_filters(0, "fb_codes0")
-        cast_filters(1)
-        quantise_filters(1, "fb_codes1")
+        squares_by_half("im", 0, 0, "raw_re00", WIDE)
+        squares_by_half("im", 0, 1, "raw_re10", BANK)
+        chunks = [(h, lo) for h in range(2) for lo in range(0, BANK, WIDE)]
+        for number, (h, lo) in enumerate(chunks):
+            add_squares(0, h, lo, WIDE)
+            if number > 0:
+                quantise_weight(*shared[number - 1], 2, 2)
+            quantise_power(0, h, lo, WIDE)
+        for g in range(2):
+            cast_filters(g)
+            quantise_filters(g)
 
-        squares_by_half("re", 1, 0, "raw_im00", 0, [BANK])
-        squares_by_half("re", 1, 1, "raw_im10", 1, [BANK])
-        squares_by_half("im", 1, 0, "late_squares", 0, [WIDE, WIDE])
-        squares_by_half("im", 1, 1, "raw_re01", 1, [WIDE, WIDE])
-        add_squares(1, 0, 0, WIDE, "power0")
-        quantise_power(1, 0, 0, WIDE)
-        filter_bank(0, WIDE, 0)
-        add_squares(1, 0, WIDE, WIDE, "power1")
-        quantise_power(1, 0, WIDE, WIDE)
-        filter_bank(WIDE, WIDE, 1)
-        for lo in range(0, BANK, NARROW):
-            add_squares(1, 1, lo, NARROW, "power2%d" % lo)
-            quantise_power(1, 1, lo, NARROW)
-            if lo < WIDE:
-                filter_bank(BANK + lo, NARROW, 2 + lo // NARROW)
-            else:
-                split_filter_bank(BANK + lo, NARROW, 2 * (lo // NARROW))
+        squares_by_half("re", 1, 0, "raw_im00", BANK)
+        squares_by_half("re", 1, 1, "raw_im10", BANK)
+        squares_by_half("im", 1, 0, "late_squares", WIDE)
+        squares_by_half("im", 1, 1, "raw_re01", WIDE)
+        bank = 0
+        for h, width in enumerate((WIDE, NARROW)):
+            for lo in range(0, BANK, width):
+                add_squares(1, h, lo, width)
+                quantise_power(1, h, lo, width)
+                if h * BANK + lo < J - 2 * NARROW:
+                    filter_bank(h * BANK + lo, width, bank)
+                    bank = bank + 1
+                else:
+                    split_filter_bank(h * BANK + lo, width, bank)
+                    bank = bank + 2

@@ -32,7 +32,7 @@ def tile_list_meltab_pow_kernel(tc, tab_words, tab_scales, co, si, gn, fb, offs,
         psum = ctx.enter_context(tc.psum_pool(name="psum", bufs=1))
 
         def sbuf(shape, dtype, slot):
-            return keep.tile(shape, dtype, name=slot, align_bytes=64)
+            return keep.tile(shape, dtype, name=slot, align_bytes=256)
 
         def copy(engine, dst, src):
             if engine == "scalar":

@@ -88,7 +88,7 @@ def tile_list_meltab_pow_kernel(tc, tab_words, tab_scales, co, si, gn, fb, offs,
         def load_gain():
             runs = gn.rearrange("(g q e) -> q g e", g=2, e=2 * PACK)
             for r in range(2):
-                nc.sync.dma_start(out=gain[r:P:2, :, :6], in_=runs[:, :, 2 * r : 2 * r + 6])
+                nc.scalar.dma_start(out=gain[r:P:2, :, :6], in_=runs[:, :, 2 * r : 2 * r + 6])
 
         def prepare_gain():
             own = gain[:].rearrange("p g (u e) -> p (g u) e", u=2)[:, :, :2]
@@ -97,10 +97,10 @@ def tile_list_meltab_pow_kernel(tc, tab_words, tab_scales, co, si, gn, fb, offs,
             half = keep.tile([P, 2 * PACK], F32, name="half")
             pairs = sign[:].rearrange("p g (u s) -> p (g u) s", u=2)
             nc.gpsimd.memset(half[:], 0.5)
-            nc.gpsimd.tensor_scalar(out=twice[:], in0=own, scalar1=0.0, scalar2=2.0, op0=ALU.is_ge, op1=ALU.mult)
-            nc.gpsimd.tensor_scalar(out=pairs, in0=twice[:], scalar1=-1.0, scalar2=None, op0=ALU.add)
-            nc.gpsimd.tensor_tensor(out=size[:], in0=own, in1=pairs, op=ALU.mult)
+            nc.vector.scalar_tensor_tensor(out=size[:], in0=own, scalar=-1.0, in1=own, op0=ALU.mult, op1=ALU.max)
+            nc.vector.tensor_scalar(out=twice[:], in0=own, scalar1=0.0, scalar2=2.0, op0=ALU.is_ge, op1=ALU.mult)
             nc.gpsimd.tensor_tensor(out=root[:], in0=size[:].rearrange("p x s -> p (x s)"), in1=half[:], op=ALU.pow)
+            nc.gpsimd.tensor_scalar(out=pairs, in0=twice[:], scalar1=-1.0, scalar2=None, op0=ALU.add)
 
 
         def load(part, a, g):
@@ -248,13 +248,13 @@ def tile_list_meltab_pow_kernel(tc, tab_words, tab_scales, co, si, gn, fb, offs,
 
         nc.vector.memset(scale_store[:], 0)
         nc.vector.memset(frame_scales[:].bitcast(I32), 0)
+        load_gain()
+        prepare_gain()
         load_table(0, FIRST)
         nc.sync.dma_start(offsets[:], offs)
         load_scales()
-        load_gain()
         load_table(FIRST, T)
         load("re", 0, 0)
-        prepare_gain()
         gather_scales()
         load("re", 1, 0)
         load("im", 0, 0)

@@ -103,18 +103,25 @@ def tile_list_meltab_pow_kernel(tc, tab_words, tab_scales, co, si, gn, fb, offs,
             nc.gpsimd.tensor_scalar(out=pairs, in0=twice[:], scalar1=-1.0, scalar2=None, op0=ALU.add)
 
 
-        def load(part, a, g):
-            tile = sbuf([P, PACK, BANK], F32, "raw_%s%d%d" % (part, a, g))
-            rows = weights[part][a * PASS : (a + 1) * PASS, g * BANK : (g + 1) * BANK]
-            nc.sync.dma_start(out=tile[:], in_=rows.rearrange("(p i) f -> p i f", i=PACK))
+        def load(part, a, g, cuts=1):
+            width = BANK // cuts
+            tile = sbuf([P, cuts, PACK, width], F32, "raw_%s%d%d" % (part, a, g))
+            for cut in range(cuts):
+                lo = g * BANK + cut * width
+                rows = weights[part][a * PASS : (a + 1) * PASS, lo : lo + width]
+                nc.sync.dma_start(out=tile[:, cut], in_=rows.rearrange("(p i) f -> p i f", i=PACK))
             raw[part, a, g] = tile
 
-        def cast(part, a, g, first, count, engine):
-            tile = sbuf([P, count * BANK], BF16, "rounded_%s%d%d%d" % (part, a, g, first))
+        def cast(part, a, g, first, count, engine, cut=0, cuts=1):
+            if cut == 0:
+                tile = sbuf([P, count * BANK], BF16, "rounded_%s%d%d%d" % (part, a, g, first))
+            else:
+                tile = rounded[part, a, g, first][0]
             u, s = divmod(first, 2)
+            share = P // 2 // cuts
             dst = tile[:].rearrange("p (s q r i) -> p q i r s", s=count, r=2, i=PACK)
-            src = raw[part, a, g][:].rearrange("p i (q u r s) -> p u q i r s", u=2, r=2, s=2)
-            copy(engine, dst, src[:, u, :, :, :, s : s + count])
+            src = raw[part, a, g][:, cut].rearrange("p i (q u r s) -> p u q i r s", u=2, r=2, s=2)
+            copy(engine, dst[:, cut * share : (cut + 1) * share], src[:, u, :, :, :, s : s + count])
             for t in range(count):
                 rounded[part, a, g, first + t] = (tile, t)
 
@@ -128,61 +135,68 @@ def tile_list_meltab_pow_kernel(tc, tab_words, tab_scales, co, si, gn, fb, offs,
                 cols = slice(t * P, (t + 1) * P)
                 w_codes[part, a, g, first + t], w_scales[part, a, g, first + t] = codes[:, cols], scales[:, cols]
 
-        def vector_piece(part, a, g):
-            cast(part, a, g, 0, 2, "vector")
-            cast(part, a, g, 2, 2, "vector")
+        def vector_piece(part, a, g, cuts=1):
+            for cut in range(cuts):
+                cast(part, a, g, 0, 2, "vector", cut, cuts)
+                cast(part, a, g, 2, 2, "vector", cut, cuts)
             quantise_weight(part, a, g, 0, 2)
             quantise_weight(part, a, g, 2, 2)
 
-        def shared_piece(part, a, g):
-            cast(part, a, g, 0, 2, "vector")
-            cast(part, a, g, 2, 2, "scalar")
-            quantise_weight(part, a, g, 0, 2)
 
-
-        def transform(part, g, h, t, bank, lead):
-            sums[t] = psum.tile([P, BANK], F32, name="bank%d" % bank)
-            for a in (lead, 1 - lead):
-                nc.tensor.matmul_mx(
-                    out=sums[t][:],
-                    lhsT=w_codes[part, a, g, t].bitcast(FP8X4),
-                    lhsT_scale=w_scales[part, a, g, t],
-                    rhs=frames[h][:, a, :].bitcast(FP4X4),
-                    rhs_scale=frame_scales[:, a * J + h * BANK : a * J + (h + 1) * BANK],
-                    start=(a == lead),
-                    stop=(a != lead),
-                )
+        def transform(part, g, h, t, bank, a, start):
+            if start:
+                sums[t] = psum.tile([P, BANK], F32, name="bank%d" % bank)
+            nc.tensor.matmul_mx(
+                out=sums[t][:],
+                lhsT=w_codes[part, a, g, t].bitcast(FP8X4),
+                lhsT_scale=w_scales[part, a, g, t],
+                rhs=frames[h][:, a, :].bitcast(FP4X4),
+                rhs_scale=frame_scales[:, a * J + h * BANK : a * J + (h + 1) * BANK],
+                start=start,
+                stop=not start,
+            )
 
         def square(part, g, h, t, lo, width):
-            cols = slice(lo, lo + width)
+            tile, first = squared[part, g, h, lo // WIDE]
             column = PACK * g + t
-            nc.scalar.activation(out=squared[part, g, h][:, t, cols], in_=sums[t][:, cols], func=ACT.Square, scale=root[:, column : column + 1])
+            nc.scalar.activation(
+                out=tile[:, t, lo - first : lo - first + width],
+                in_=sums[t][:, lo : lo + width],
+                func=ACT.Square,
+                scale=root[:, column : column + 1],
+            )
 
         def first_squares():
             both_halves = sbuf([P, 2, PACK, BANK], F32, "word_store")
-            squared["re", 0, 0], squared["re", 0, 1] = both_halves[:, 0], both_halves[:, 1]
+            for h in range(2):
+                squared["re", 0, h, 0] = squared["re", 0, h, 1] = (both_halves[:, h], 0)
             order = [(h, t) for pair in range(2) for h in range(2) for t in (2 * pair, 2 * pair + 1)]
             for bank, (h, t) in enumerate(order):
-                transform("re", 0, h, t, bank, 0 if t < 2 else 1)
+                lead = 0 if t < 2 else 1
+                transform("re", 0, h, t, bank, lead, True)
+                transform("re", 0, h, t, bank, 1 - lead, False)
                 square("re", 0, h, t, 0, BANK)
 
-        def squares_by_half(part, g, h, slot, width):
-            squared[part, g, h] = sbuf([P, PACK, BANK], F32, slot)
-            for t in range(PACK):
-                transform(part, g, h, t, PACK * h + t, h)
+        def squares_by_half(part, g, h, slots, width):
+            for c, slot in enumerate(slots):
+                tile = sbuf([P, PACK, BANK // len(slots)], F32, slot)
+                squared[part, g, h, c] = (tile, c * WIDE)
+            if len(slots) == 1:
+                squared[part, g, h, 1] = squared[part, g, h, 0]
+            for a in (h, 1 - h):
+                for t in range(PACK):
+                    transform(part, g, h, t, PACK * h + t, a, a == h)
             for lo in range(0, BANK, width):
                 for t in range(PACK):
                     square(part, g, h, t, lo, width)
 
         def add_squares(g, h, lo, width):
             tile = sbuf([P, PACK * width], BF16, "power%d%d_%d" % (g, h, lo))
-            cols = slice(lo, lo + width)
-            nc.vector.tensor_tensor(
-                out=tile[:].rearrange("p (c i t) -> p c t i", i=4, t=PACK),
-                in0=squared["re", g, h][:, :, cols].rearrange("p t (c i) -> p c t i", i=4),
-                in1=squared["im", g, h][:, :, cols].rearrange("p t (c i) -> p c t i", i=4),
-                op=ALU.add,
-            )
+            both = []
+            for part in ("re", "im"):
+                source, first = squared[part, g, h, lo // WIDE]
+                both.append(source[:, :, lo - first : lo - first + width].rearrange("p t (c i) -> p c t i", i=4))
+            nc.vector.tensor_tensor(out=tile[:].rearrange("p (c i t) -> p c t i", i=4, t=PACK), in0=both[0], in1=both[1], op=ALU.add)
             power[g, h, lo] = tile
 
         def quantise_power(g, h, lo, width):
@@ -258,8 +272,8 @@ def tile_list_meltab_pow_kernel(tc, tab_words, tab_scales, co, si, gn, fb, offs,
         gather_scales()
         load("re", 1, 0)
         load("im", 0, 0)
-        load("im", 1, 0)
-        load("re", 0, 1)
+        load("im", 1, 0, 2)
+        load("re", 0, 1, 2)
         load("re", 1, 1)
         load("im", 0, 1)
         load("im", 1, 1)
@@ -284,29 +298,36 @@ def tile_list_meltab_pow_kernel(tc, tab_words, tab_scales, co, si, gn, fb, offs,
         quantise_weight("re", 1, 0, 2, 2)
         first_squares()
 
-        shared = [("re", 1, 1), ("im", 0, 1), ("im", 1, 1)]
         vector_piece("im", 0, 0)
-        vector_piece("im", 1, 0)
-        vector_piece("re", 0, 1)
-        for piece in shared:
-            shared_piece(*piece)
-
-        squares_by_half("im", 0, 0, "raw_re00", WIDE)
-        squares_by_half("im", 0, 1, "raw_re10", BANK)
-        chunks = [(h, lo) for h in range(2) for lo in range(0, BANK, WIDE)]
-        for number, (h, lo) in enumerate(chunks):
-            add_squares(0, h, lo, WIDE)
-            if number > 0:
-                quantise_weight(*shared[number - 1], 2, 2)
-            quantise_power(0, h, lo, WIDE)
+        vector_piece("im", 1, 0, 2)
+        vector_piece("re", 0, 1, 2)
+        squares_by_half("im", 0, 0, ["raw_re00"], WIDE)
+        cast("re", 1, 1, 0, 2, "scalar")
+        cast("re", 1, 1, 2, 2, "scalar")
+        cast("im", 1, 1, 2, 2, "scalar")
+        add_squares(0, 0, 0, WIDE)
+        add_squares(0, 0, WIDE, WIDE)
+        quantise_weight("re", 1, 1, 0, 2)
+        squares_by_half("im", 0, 1, ["raw_re10", "rounded_re110"], WIDE)
+        add_squares(0, 1, 0, WIDE)
+        quantise_power(0, 0, 0, WIDE)
+        quantise_power(0, 0, WIDE, WIDE)
+        quantise_power(0, 1, 0, WIDE)
+        quantise_weight("re", 1, 1, 2, 2)
+        vector_piece("im", 0, 1)
+        cast("im", 1, 1, 0, 2, "vector")
+        add_squares(0, 1, WIDE, WIDE)
+        quantise_weight("im", 1, 1, 0, 2)
+        quantise_power(0, 1, WIDE, WIDE)
+        quantise_weight("im", 1, 1, 2, 2)
         for g in range(2):
             cast_filters(g)
             quantise_filters(g)
 
-        squares_by_half("re", 1, 0, "raw_im00", BANK)
-        squares_by_half("re", 1, 1, "raw_im10", BANK)
-        squares_by_half("im", 1, 0, "late_squares", WIDE)
-        squares_by_half("im", 1, 1, "raw_re01", WIDE)
+        squares_by_half("re", 1, 0, ["raw_im00"], BANK)
+        squares_by_half("re", 1, 1, ["raw_im10"], BANK)
+        squares_by_half("im", 1, 0, ["late_squares"], WIDE)
+        squares_by_half("im", 1, 1, ["raw_re01"], WIDE)
         bank = 0
         for h, width in enumerate((WIDE, NARROW)):
             for lo in range(0, BANK, width):

@@ -51,6 +51,7 @@ def tile_list_meltab_pow_kernel(tc, tab_words, tab_scales, co, si, gn, fb, offs,
         sign = keep.tile([P, 2, PACK], F32, name="sign")
         h_codes = [sbuf([P, J], U32, "h_codes%d" % g) for g in range(2)]
         h_scales = [sbuf([P, J], U8, "h_scales%d" % g) for g in range(2)]
+        rounded_fb = sbuf([P, 2, PACK * N], BF16, "rounded_fb")
         weights = {"re": co, "im": si}
         raw, rounded, w_codes, w_scales = {}, {}, {}, {}
         frames, sums, squared, power, fb_codes, fb_scales = {}, {}, {}, {}, {}, {}
@@ -112,18 +113,21 @@ def tile_list_meltab_pow_kernel(tc, tab_words, tab_scales, co, si, gn, fb, offs,
                 nc.sync.dma_start(out=tile[:, cut], in_=rows.rearrange("(p i) f -> p i f", i=PACK))
             raw[part, a, g] = tile
 
-        def cast(part, a, g, first, count, engine, cut=0, cuts=1):
-            if cut == 0:
-                tile = sbuf([P, count * BANK], BF16, "rounded_%s%d%d%d" % (part, a, g, first))
-            else:
-                tile = rounded[part, a, g, first][0]
+        def cast(part, a, g, first, count, engine, cut=0, cuts=1, whole=False):
+            if whole and (part, a, g, 0) not in rounded:
+                piece = sbuf([P, PACK * BANK], BF16, "rounded_%s%d%d" % (part, a, g))
+                for t in range(PACK):
+                    rounded[part, a, g, t] = (piece, t)
+            if (part, a, g, first) not in rounded:
+                own = sbuf([P, count * BANK], BF16, "rounded_%s%d%d%d" % (part, a, g, first))
+                for t in range(count):
+                    rounded[part, a, g, first + t] = (own, t)
+            tile, place = rounded[part, a, g, first]
             u, s = divmod(first, 2)
             share = P // 2 // cuts
-            dst = tile[:].rearrange("p (s q r i) -> p q i r s", s=count, r=2, i=PACK)
+            dst = tile[:, place * BANK : (place + count) * BANK].rearrange("p (s q r i) -> p q i r s", s=count, r=2, i=PACK)
             src = raw[part, a, g][:, cut].rearrange("p i (q u r s) -> p u q i r s", u=2, r=2, s=2)
             copy(engine, dst[:, cut * share : (cut + 1) * share], src[:, u, :, :, :, s : s + count])
-            for t in range(count):
-                rounded[part, a, g, first + t] = (tile, t)
 
         def quantise_weight(part, a, g, first, count, slot=None):
             name = "%s%d%d%d" % (part, a, g, first)
@@ -134,6 +138,11 @@ def tile_list_meltab_pow_kernel(tc, tab_words, tab_scales, co, si, gn, fb, offs,
             for t in range(count):
                 cols = slice(t * P, (t + 1) * P)
                 w_codes[part, a, g, first + t], w_scales[part, a, g, first + t] = codes[:, cols], scales[:, cols]
+
+        def whole_piece(part, a, g, cuts=1):
+            for cut in range(cuts):
+                cast(part, a, g, 0, 2, "vector", cut, cuts, True)
+                cast(part, a, g, 2, 2, "vector", cut, cuts, True)
 
         def vector_piece(part, a, g, cuts=1):
             for cut in range(cuts):
@@ -177,7 +186,7 @@ def tile_list_meltab_pow_kernel(tc, tab_words, tab_scales, co, si, gn, fb, offs,
                 transform("re", 0, h, t, bank, 1 - lead, False)
                 square("re", 0, h, t, 0, BANK)
 
-        def squares_by_half(part, g, h, slots, width):
+        def squares_by_half(part, g, h, slots, width, banks):
             for c, slot in enumerate(slots):
                 tile = sbuf([P, PACK, BANK // len(slots)], F32, slot)
                 squared[part, g, h, c] = (tile, c * WIDE)
@@ -185,19 +194,24 @@ def tile_list_meltab_pow_kernel(tc, tab_words, tab_scales, co, si, gn, fb, offs,
                 squared[part, g, h, 1] = squared[part, g, h, 0]
             for a in (h, 1 - h):
                 for t in range(PACK):
-                    transform(part, g, h, t, PACK * h + t, a, a == h)
+                    transform(part, g, h, t, banks[t], a, a == h)
             for lo in range(0, BANK, width):
                 for t in range(PACK):
                     square(part, g, h, t, lo, width)
 
         def add_squares(g, h, lo, width):
-            tile = sbuf([P, PACK * width], BF16, "power%d%d_%d" % (g, h, lo))
+            if g == 0:
+                if lo == 0:
+                    power[g, h, 0] = sbuf([P, PACK * BANK], BF16, "power%d%d" % (g, h))
+                tile = power[g, h, 0][:, PACK * lo : PACK * (lo + width)]
+            else:
+                power[g, h, lo] = sbuf([P, PACK * width], BF16, "power%d%d_%d" % (g, h, lo))
+                tile = power[g, h, lo][:]
             both = []
             for part in ("re", "im"):
                 source, first = squared[part, g, h, lo // WIDE]
                 both.append(source[:, :, lo - first : lo - first + width].rearrange("p t (c i) -> p c t i", i=4))
-            nc.vector.tensor_tensor(out=tile[:].rearrange("p (c i t) -> p c t i", i=4, t=PACK), in0=both[0], in1=both[1], op=ALU.add)
-            power[g, h, lo] = tile
+            nc.vector.tensor_tensor(out=tile.rearrange("p (c i t) -> p c t i", i=4, t=PACK), in0=both[0], in1=both[1], op=ALU.add)
 
         def quantise_power(g, h, lo, width):
             cols = slice(h * BANK + lo, h * BANK + lo + width)
@@ -212,19 +226,19 @@ def tile_list_meltab_pow_kernel(tc, tab_words, tab_scales, co, si, gn, fb, offs,
             raw["fb", g] = tile
 
         def cast_filters(g):
-            tile = sbuf([P, PACK * N], BF16, "rounded_fb%d" % g)
             nc.vector.tensor_tensor(
-                out=tile[:].rearrange("p (c i t) -> p c t i", i=4, t=PACK),
+                out=rounded_fb[:, g, :].rearrange("p (c i t) -> p c t i", i=4, t=PACK),
                 in0=raw["fb", g][:].rearrange("p t (c i) -> p c t i", i=4),
                 in1=sign[:, g, :].unsqueeze(1).unsqueeze(3).to_broadcast([P, N // 4, PACK, 4]),
                 op=ALU.mult,
             )
-            rounded["fb", g] = tile
 
-        def quantise_filters(g):
-            fb_codes[g] = sbuf([P, N], U32, "fb_codes%d" % g)
-            fb_scales[g] = sbuf([P, N], U8, "fb_scales%d" % g)
-            nc.vector.quantize_mx(out=fb_codes[g][:].bitcast(FP8X4), scales=fb_scales[g][:], in_=rounded["fb", g][:])
+        def quantise_filters():
+            codes = sbuf([P, 2 * N], U32, "fb_codes")
+            scales = sbuf([P, 2 * N], U8, "fb_scales")
+            nc.vector.quantize_mx(out=codes[:].bitcast(FP8X4), scales=scales[:], in_=rounded_fb[:].rearrange("p g x -> p (g x)"))
+            for g in range(2):
+                fb_codes[g], fb_scales[g] = codes[:, g * N : (g + 1) * N], scales[:, g * N : (g + 1) * N]
 
         def filter_pass(total, g, b, cols, start, stop):
             rows = slice(b * P, (b + 1) * P)
@@ -301,41 +315,44 @@ def tile_list_meltab_pow_kernel(tc, tab_words, tab_scales, co, si, gn, fb, offs,
         vector_piece("im", 0, 0)
         vector_piece("im", 1, 0, 2)
         vector_piece("re", 0, 1, 2)
-        squares_by_half("im", 0, 0, ["raw_re00"], WIDE)
+        squares_by_half("im", 0, 0, ["raw_re00"], WIDE, (0, 1, 2, 3))
         cast("re", 1, 1, 0, 2, "scalar")
         cast("re", 1, 1, 2, 2, "scalar")
         cast("im", 1, 1, 2, 2, "scalar")
         add_squares(0, 0, 0, WIDE)
         add_squares(0, 0, WIDE, WIDE)
         quantise_weight("re", 1, 1, 0, 2)
-        squares_by_half("im", 0, 1, ["raw_re10", "rounded_re110"], WIDE)
+        squares_by_half("im", 0, 1, ["raw_re10", "rounded_re110"], WIDE, (4, 5, 6, 7))
         add_squares(0, 1, 0, WIDE)
-        quantise_power(0, 0, 0, WIDE)
-        quantise_power(0, 0, WIDE, WIDE)
-        quantise_power(0, 1, 0, WIDE)
+        quantise_power(0, 0, 0, BANK)
         quantise_weight("re", 1, 1, 2, 2)
-        vector_piece("im", 0, 1)
+        whole_piece("im", 0, 1)
         cast("im", 1, 1, 0, 2, "vector")
         add_squares(0, 1, WIDE, WIDE)
+        quantise_weight("im", 0, 1, 0, PACK)
         quantise_weight("im", 1, 1, 0, 2)
-        quantise_power(0, 1, WIDE, WIDE)
         quantise_weight("im", 1, 1, 2, 2)
+        quantise_power(0, 1, 0, BANK)
         for g in range(2):
             cast_filters(g)
-            quantise_filters(g)
 
-        squares_by_half("re", 1, 0, ["raw_im00"], BANK)
-        squares_by_half("re", 1, 1, ["raw_im10"], BANK)
-        squares_by_half("im", 1, 0, ["late_squares"], WIDE)
-        squares_by_half("im", 1, 1, ["raw_re01"], WIDE)
-        bank = 0
-        for h, width in enumerate((WIDE, NARROW)):
-            for lo in range(0, BANK, width):
-                add_squares(1, h, lo, width)
-                quantise_power(1, h, lo, width)
-                if h * BANK + lo < J - 2 * NARROW:
-                    filter_bank(h * BANK + lo, width, bank)
-                    bank = bank + 1
-                else:
-                    split_filter_bank(h * BANK + lo, width, bank)
-                    bank = bank + 2
+        squares_by_half("re", 1, 0, ["raw_im00"], BANK, (0, 1, 2, 3))
+        squares_by_half("im", 1, 0, ["late_squares"], WIDE, (0, 1, 2, 3))
+        squares_by_half("re", 1, 1, ["raw_im10"], BANK, (4, 5, 6, 7))
+        squares_by_half("im", 1, 1, ["raw_re01"], WIDE, (4, 5, 0, 1))
+        add_squares(1, 0, 0, WIDE)
+        quantise_filters()
+        quantise_power(1, 0, 0, WIDE)
+        filter_bank(0, WIDE, 2)
+        add_squares(1, 0, WIDE, WIDE)
+        add_squares(1, 1, 0, NARROW)
+        quantise_power(1, 0, WIDE, WIDE)
+        filter_bank(WIDE, WIDE, 3)
+        for lo, bank in zip(range(0, BANK, NARROW), (6, 7, 4, 0)):
+            if lo > 0:
+                add_squares(1, 1, lo, NARROW)
+            quantise_power(1, 1, lo, NARROW)
+            if lo < BANK - 2 * NARROW:
+                filter_bank(BANK + lo, NARROW, bank)
+            else:
+                split_filter_bank(BANK + lo, NARROW, bank)

@@ -233,12 +233,10 @@ def tile_list_meltab_pow_kernel(tc, tab_words, tab_scales, co, si, gn, fb, offs,
                 op=ALU.mult,
             )
 
-        def quantise_filters():
-            codes = sbuf([P, 2 * N], U32, "fb_codes")
-            scales = sbuf([P, 2 * N], U8, "fb_scales")
-            nc.vector.quantize_mx(out=codes[:].bitcast(FP8X4), scales=scales[:], in_=rounded_fb[:].rearrange("p g x -> p (g x)"))
-            for g in range(2):
-                fb_codes[g], fb_scales[g] = codes[:, g * N : (g + 1) * N], scales[:, g * N : (g + 1) * N]
+        def quantise_filters(g):
+            fb_codes[g] = sbuf([P, N], U32, "fb_codes%d" % g)
+            fb_scales[g] = sbuf([P, N], U8, "fb_scales%d" % g)
+            nc.vector.quantize_mx(out=fb_codes[g][:].bitcast(FP8X4), scales=fb_scales[g][:], in_=rounded_fb[:, g, :])
 
         def filter_pass(total, g, b, cols, start, stop):
             rows = slice(b * P, (b + 1) * P)
@@ -260,6 +258,17 @@ def tile_list_meltab_pow_kernel(tc, tab_words, tab_scales, co, si, gn, fb, offs,
                 for b in range(2):
                     filter_pass(total[:, b, :], g, b, cols, g == 0 and b == 0, g == 1 and b == 1)
             copy("scalar", result[:], total[:])
+            nc.sync.dma_start(out=out.rearrange("(b p) j -> p b j", p=P)[:, :, cols], in_=result[:])
+
+        def two_bank_filter(lo, width, banks):
+            cols = slice(lo, lo + width)
+            totals = [psum.tile([P, width], F32, name="bank%d" % bank) for bank in banks]
+            for g in range(2):
+                for b in range(2):
+                    filter_pass(totals[b][:], g, b, cols, g == 0, g == 1)
+            result = sbuf([P, 2, width], F32, "result%d" % lo)
+            for b in range(2):
+                copy("scalar", result[:, b, :], totals[b][:])
             nc.sync.dma_start(out=out.rearrange("(b p) j -> p b j", p=P)[:, :, cols], in_=result[:])
 
         def split_filter_bank(lo, width, first_bank):
@@ -339,16 +348,17 @@ def tile_list_meltab_pow_kernel(tc, tab_words, tab_scales, co, si, gn, fb, offs,
         squares_by_half("re", 1, 0, ["raw_im00"], BANK, (0, 1, 2, 3))
         squares_by_half("im", 1, 0, ["late_squares"], WIDE, (0, 1, 2, 3))
         squares_by_half("re", 1, 1, ["raw_im10"], BANK, (4, 5, 6, 7))
-        squares_by_half("im", 1, 1, ["raw_re01"], WIDE, (4, 5, 0, 1))
+        quantise_filters(0)
         add_squares(1, 0, 0, WIDE)
-        quantise_filters()
+        quantise_filters(1)
         quantise_power(1, 0, 0, WIDE)
         filter_bank(0, WIDE, 2)
+        squares_by_half("im", 1, 1, ["raw_re01"], WIDE, (4, 5, 0, 1))
         add_squares(1, 0, WIDE, WIDE)
         add_squares(1, 1, 0, NARROW)
         quantise_power(1, 0, WIDE, WIDE)
-        filter_bank(WIDE, WIDE, 3)
-        for lo, bank in zip(range(0, BANK, NARROW), (6, 7, 4, 0)):
+        two_bank_filter(WIDE, WIDE, (3, 7))
+        for lo, bank in zip(range(0, BANK, NARROW), (6, 2, 4, 0)):
             if lo > 0:
                 add_squares(1, 1, lo, NARROW)
             quantise_power(1, 1, lo, NARROW)

from contextlib import ExitStack

import concourse.mybir as mybir

K, F, N, T, J = 1024, 1024, 256, 4096, 1024
FLOPS = 2 * (2 * K * F * J + F * N * J)

F32 = mybir.dt.float32
BF16 = mybir.dt.bfloat16
I32 = mybir.dt.int32
U32 = mybir.dt.uint32
U16 = mybir.dt.uint16
U8 = mybir.dt.uint8
FP8X4 = mybir.dt.float8_e4m3fn_x4
FP4X4 = mybir.dt.float4_e2m1fn_x4
ALU = mybir.AluOpType
ACT = mybir.ActivationFunctionType

P = 128
PACK = 4
PASS = P * PACK
BANK = 512
WIDE = 256
NARROW = 128
FIRST = 3 * T // 8


def tile_list_meltab_pow_kernel(tc, tab_words, tab_scales, co, si, gn, fb, offs, out):
    nc = tc.nc
    with ExitStack() as ctx:
        keep = ctx.enter_context(tc.tile_pool(name="keep", bufs=1))
        psum = ctx.enter_context(tc.psum_pool(name="psum", bufs=1))

        def sbuf(shape, dtype, slot):
            return keep.tile(shape, dtype, name=slot, align_bytes=256)

        def copy(engine, dst, src):
            if engine == "scalar":
                nc.scalar.copy(out=dst, in_=src)
            else:
                nc.vector.tensor_copy(out=dst, in_=src)

        offsets = keep.tile([P, J // 16], U16, name="offsets")
        scale_store = sbuf([P, T // 4], I32, "scale_store")
        word_store = sbuf([P, T], I32, "word_store")
        picked_scales = sbuf([P, J], U8, "picked_scales")
        frame_scales = sbuf([P, 2 * J], U8, "frame_scales")
        picked_words = [sbuf([P, BANK], U32, "picked_words%d" % h) for h in range(2)]
        gain = keep.tile([P, 2, 2 * PACK], F32, name="gain")
        root = keep.tile([P, 2 * PACK], F32, name="root")
        sign = keep.tile([P, 2, PACK], F32, name="sign")
        h_codes = [sbuf([P, J], U32, "h_codes%d" % g) for g in range(2)]
        h_scales = [sbuf([P, J], U8, "h_scales%d" % g) for g in range(2)]
        rounded_fb = sbuf([P, 2, PACK * N], BF16, "rounded_fb")
        weights = {"re": co, "im": si}
        raw, rounded, w_codes, w_scales = {}, {}, {}, {}
        frames, sums, squared, power, fb_codes, fb_scales = {}, {}, {}, {}, {}, {}


        def load_table(first, last):
            words = tab_words[0].rearrange("p t b -> p (t b)").bitcast(I32)
            nc.sync.dma_start(out=word_store[:, first:last], in_=words[:, first:last])

        def load_scales():
            rows = tab_scales.bitcast(I32).rearrange("a m t -> m a t")
            nc.sync.dma_start(out=scale_store[0:P:4, :], in_=rows)

        def gather_scales():
            nc.vector.tensor_copy(picked_scales[:], scale_store[:].bitcast(U8).indirect(offsets[:]))
            for quadrant in (0, 2, 1, 3):
                first = 32 * quadrant
                nc.sync.dma_start(
                    out=frame_scales[first : first + 4, :].bitcast(I32),
                    in_=picked_scales[first : first + 32 : 4, :].bitcast(I32),
                )

        def gather_words(h):
            window = word_store[:].bitcast(U32)
            nc.vector.tensor_copy(picked_words[h][:], window.indirect(offsets[:, 32 * h : 32 * (h + 1)]))

        def part_words(h, slot):
            frames[h] = sbuf([P, 2, 2 * BANK], U8, slot)
            nc.vector.tensor_copy(
                out=frames[h][:].bitcast(U16),
                in_=picked_words[h][:].bitcast(U16).rearrange("p (j a) -> p a j", a=2),
            )


        def load_gain():
            runs = gn.rearrange("(g q e) -> q g e", g=2, e=2 * PACK)
            for r in range(2):
                nc.scalar.dma_start(out=gain[r:P:2, :, :6], in_=runs[:, :, 2 * r : 2 * r + 6])

        def prepare_gain():
            own = gain[:].rearrange("p g (u e) -> p (g u) e", u=2)[:, :, :2]
            twice = keep.tile([P, PACK, 2], F32, name="twice")
            size = keep.tile([P, PACK, 2], F32, name="size")
            half = keep.tile([P, 2 * PACK], F32, name="half")
            pairs = sign[:].rearrange("p g (u s) -> p (g u) s", u=2)
            nc.gpsimd.memset(half[:], 0.5)
            nc.vector.scalar_tensor_tensor(out=size[:], in0=own, scalar=-1.0, in1=own, op0=ALU.mult, op1=ALU.max)
            nc.vector.tensor_scalar(out=twice[:], in0=own, scalar1=0.0, scalar2=2.0, op0=ALU.is_ge, op1=ALU.mult)
            nc.gpsimd.tensor_tensor(out=root[:], in0=size[:].rearrange("p x s -> p (x s)"), in1=half[:], op=ALU.pow)
            nc.gpsimd.tensor_scalar(out=pairs, in0=twice[:], scalar1=-1.0, scalar2=None, op0=ALU.add)


        def load(part, a, g, cuts=1):
            width = BANK // cuts
            tile = sbuf([P, cuts, PACK, width], F32, "raw_%s%d%d" % (part, a, g))
            for cut in range(cuts):
                lo = g * BANK + cut * width
                rows = weights[part][a * PASS : (a + 1) * PASS, lo : lo + width]
                nc.sync.dma_start(out=tile[:, cut], in_=rows.rearrange("(p i) f -> p i f", i=PACK))
            raw[part, a, g] = tile

        def cast(part, a, g, first, count, engine, cut=0, cuts=1, whole=False):
            if whole and (part, a, g, 0) not in rounded:
                piece = sbuf([P, PACK * BANK], BF16, "rounded_%s%d%d" % (part, a, g))
                for t in range(PACK):
                    rounded[part, a, g, t] = (piece, t)
            if (part, a, g, first) not in rounded:
                own = sbuf([P, count * BANK], BF16, "rounded_%s%d%d%d" % (part, a, g, first))
                for t in range(count):
                    rounded[part, a, g, first + t] = (own, t)
            tile, place = rounded[part, a, g, first]
            u, s = divmod(first, 2)
            share = P // 2 // cuts
            dst = tile[:, place * BANK : (place + count) * BANK].rearrange("p (s q r i) -> p q i r s", s=count, r=2, i=PACK)
            src = raw[part, a, g][:, cut].rearrange("p i (q u r s) -> p u q i r s", u=2, r=2, s=2)
            copy(engine, dst[:, cut * share : (cut + 1) * share], src[:, u, :, :, :, s : s + count])

        def quantise_weight(part, a, g, first, count, slot=None):
            name = "%s%d%d%d" % (part, a, g, first)
            codes = sbuf([P, count * P], U32, slot or "w_codes_" + name)
            scales = sbuf([P, count * P], U8, "w_scales_" + name)
            tile, place = rounded[part, a, g, first]
            nc.vector.quantize_mx(out=codes[:].bitcast(FP8X4), scales=scales[:], in_=tile[:, place * BANK : (place + count) * BANK])
            for t in range(count):
                cols = slice(t * P, (t + 1) * P)
                w_codes[part, a, g, first + t], w_scales[part, a, g, first + t] = codes[:, cols], scales[:, cols]

        def whole_piece(part, a, g, cuts=1):
            for cut in range(cuts):
                cast(part, a, g, 0, 2, "vector", cut, cuts, True)
                cast(part, a, g, 2, 2, "vector", cut, cuts, True)

        def vector_piece(part, a, g, cuts=1):
            for cut in range(cuts):
                cast(part, a, g, 0, 2, "vector", cut, cuts)
                cast(part, a, g, 2, 2, "vector", cut, cuts)
            quantise_weight(part, a, g, 0, 2)
            quantise_weight(part, a, g, 2, 2)


        def transform(part, g, h, t, bank, a, start):
            if start:
                sums[t] = psum.tile([P, BANK], F32, name="bank%d" % bank)
            nc.tensor.matmul_mx(
                out=sums[t][:],
                lhsT=w_codes[part, a, g, t].bitcast(FP8X4),
                lhsT_scale=w_scales[part, a, g, t],
                rhs=frames[h][:, a, :].bitcast(FP4X4),
                rhs_scale=frame_scales[:, a * J + h * BANK : a * J + (h + 1) * BANK],
                start=start,
                stop=not start,
            )

        def square(part, g, h, t, lo, width):
            tile, first = squared[part, g, h, lo // WIDE]
            column = PACK * g + t
            nc.scalar.activation(
                out=tile[:, t, lo - first : lo - first + width],
                in_=sums[t][:, lo : lo + width],
                func=ACT.Square,
                scale=root[:, column : column + 1],
            )

        def first_squares():
            both_halves = sbuf([P, 2, PACK, BANK], F32, "word_store")
            for h in range(2):
                squared["re", 0, h, 0] = squared["re", 0, h, 1] = (both_halves[:, h], 0)
            order = [(h, t) for pair in range(2) for h in range(2) for t in (2 * pair, 2 * pair + 1)]
            for bank, (h, t) in enumerate(order):
                lead = 0 if t < 2 else 1
                transform("re", 0, h, t, bank, lead, True)
                transform("re", 0, h, t, bank, 1 - lead, False)
                square("re", 0, h, t, 0, BANK)

        def squares_by_half(part, g, h, slots, width, banks):
            for c, slot in enumerate(slots):
                tile = sbuf([P, PACK, BANK // len(slots)], F32, slot)
                squared[part, g, h, c] = (tile, c * WIDE)
            if len(slots) == 1:
                squared[part, g, h, 1] = squared[part, g, h, 0]
            for a in (h, 1 - h):
                for t in range(PACK):
                    transform(part, g, h, t, banks[t], a, a == h)
            for lo in range(0, BANK, width):
                for t in range(PACK):
                    square(part, g, h, t, lo, width)

        def add_squares(g, h, lo, width):
            if g == 0:
                if lo == 0:
                    power[g, h, 0] = sbuf([P, PACK * BANK], BF16, "power%d%d" % (g, h))
                tile = power[g, h, 0][:, PACK * lo : PACK * (lo + width)]
            else:
                power[g, h, lo] = sbuf([P, PACK * width], BF16, "power%d%d_%d" % (g, h, lo))
                tile = power[g, h, lo][:]
            both = []
            for part in ("re", "im"):
                source, first = squared[part, g, h, lo // WIDE]
                both.append(source[:, :, lo - first : lo - first + width].rearrange("p t (c i) -> p c t i", i=4))
            nc.vector.tensor_tensor(out=tile.rearrange("p (c i t) -> p c t i", i=4, t=PACK), in0=both[0], in1=both[1], op=ALU.add)

        def quantise_power(g, h, lo, width):
            cols = slice(h * BANK + lo, h * BANK + lo + width)
            nc.vector.quantize_mx(out=h_codes[g][:, cols].bitcast(FP8X4), scales=h_scales[g][:, cols], in_=power[g, h, lo][:])


        def load_filters(g):
            tile = sbuf([P, PACK, N], F32, "raw_fb%d" % g)
            rows = fb[g * PASS : (g + 1) * PASS, :].rearrange("(q u r s) n -> u q r (s n)", u=2, r=2, s=2)
            for u in range(2):
                nc.sync.dma_start(out=tile[:, 2 * u : 2 * u + 2, :].rearrange("p s n -> p (s n)"), in_=rows[u])
            raw["fb", g] = tile

        def cast_filters(g):
            nc.vector.tensor_tensor(
                out=rounded_fb[:, g, :].rearrange("p (c i t) -> p c t i", i=4, t=PACK),
                in0=raw["fb", g][:].rearrange("p t (c i) -> p c t i", i=4),
                in1=sign[:, g, :].unsqueeze(1).unsqueeze(3).to_broadcast([P, N // 4, PACK, 4]),
                op=ALU.mult,
            )

        def quantise_filters(g):
            fb_codes[g] = sbuf([P, N], U32, "fb_codes%d" % g)
            fb_scales[g] = sbuf([P, N], U8, "fb_scales%d" % g)
            nc.vector.quantize_mx(out=fb_codes[g][:].bitcast(FP8X4), scales=fb_scales[g][:], in_=rounded_fb[:, g, :])

        def filter_pass(total, g, b, cols, start, stop):
            rows = slice(b * P, (b + 1) * P)
            nc.tensor.matmul_mx(
                out=total,
                lhsT=fb_codes[g][:, rows].bitcast(FP8X4),
                lhsT_scale=fb_scales[g][:, rows],
                rhs=h_codes[g][:, cols].bitcast(FP8X4),
                rhs_scale=h_scales[g][:, cols],
                start=start,
                stop=stop,
            )

        def filter_bank(lo, width, bank):
            cols = slice(lo, lo + width)
            result = sbuf([P, 2, width], F32, "result%d" % lo)
            total = psum.tile([P, 2, width], F32, name="bank%d" % bank)
            for g in range(2):
                for b in range(2):
                    filter_pass(total[:, b, :], g, b, cols, g == 0 and b == 0, g == 1 and b == 1)
            copy("scalar", result[:], total[:])
            nc.sync.dma_start(out=out.rearrange("(b p) j -> p b j", p=P)[:, :, cols], in_=result[:])

        def two_bank_filter(lo, width, banks):
            cols = slice(lo, lo + width)
            totals = [psum.tile([P, width], F32, name="bank%d" % bank) for bank in banks]
            for g in range(2):
                for b in range(2):
                    filter_pass(totals[b][:], g, b, cols, g == 0, g == 1)
            result = sbuf([P, 2, width], F32, "result%d" % lo)
            for b in range(2):
                copy("scalar", result[:, b, :], totals[b][:])
            nc.sync.dma_start(out=out.rearrange("(b p) j -> p b j", p=P)[:, :, cols], in_=result[:])

        def split_filter_bank(lo, width, first_bank):
            cols = slice(lo, lo + width)
            totals = [psum.tile([P, width], F32, name="bank%d" % (first_bank + b)) for b in range(2)]
            for g in range(2):
                for b in range(2):
                    filter_pass(totals[b][:], g, b, cols, g == 0, g == 1)
            result = sbuf([P, 2, width], F32, "result%d" % lo)
            copy("vector", result[:, 0, :], totals[0][:])
            nc.sync.dma_start(out=out[:P, cols], in_=result[:, 0, :])
            copy("scalar", result[:, 1, :], totals[1][:])
            nc.scalar.dma_start(out=out[P:, cols], in_=result[:, 1, :])

        nc.vector.memset(scale_store[:], 0)
        nc.vector.memset(frame_scales[:].bitcast(I32), 0)
        load_gain()
        prepare_gain()
        load_table(0, FIRST)
        nc.sync.dma_start(offsets[:], offs)
        load_scales()
        load_table(FIRST, T)
        load("re", 0, 0)
        gather_scales()
        load("re", 1, 0)
        load("im", 0, 0)
        load("im", 1, 0, 2)
        load("re", 0, 1, 2)
        load("re", 1, 1)
        load("im", 0, 1)
        load("im", 1, 1)
        load_filters(0)
        load_filters(1)

        gather_words(0)
        part_words(0, "frames0")
        gather_words(1)
        cast("re", 0, 0, 0, 1, "scalar")
        cast("re", 0, 0, 1, 1, "scalar")
        cast("re", 0, 0, 2, 2, "scalar")
        cast("re", 1, 0, 2, 2, "scalar")
        quantise_weight("re", 0, 0, 0, 1)
        part_words(1, "rounded_re000")
        quantise_weight("re", 0, 0, 1, 1)
        cast("re", 1, 0, 0, 1, "vector")
        cast("re", 1, 0, 1, 1, "vector")
        quantise_weight("re", 1, 0, 0, 1)
        quantise_weight("re", 1, 0, 1, 1)
        quantise_weight("re", 0, 0, 2, 2, "rounded_re100")
        quantise_weight("re", 1, 0, 2, 2)
        first_squares()

        vector_piece("im", 0, 0)
        vector_piece("im", 1, 0, 2)
        vector_piece("re", 0, 1, 2)
        squares_by_half("im", 0, 0, ["raw_re00"], WIDE, (0, 1, 2, 3))
        cast("re", 1, 1, 0, 2, "scalar")
        cast("re", 1, 1, 2, 2, "scalar")
        cast("im", 1, 1, 2, 2, "scalar")
        add_squares(0, 0, 0, WIDE)
        add_squares(0, 0, WIDE, WIDE)
        quantise_weight("re", 1, 1, 0, 2)
        squares_by_half("im", 0, 1, ["raw_re10", "rounded_re110"], WIDE, (4, 5, 6, 7))
        add_squares(0, 1, 0, WIDE)
        quantise_power(0, 0, 0, BANK)
        quantise_weight("re", 1, 1, 2, 2)
        whole_piece("im", 0, 1)
        cast("im", 1, 1, 0, 2, "vector")
        add_squares(0, 1, WIDE, WIDE)
        quantise_weight("im", 0, 1, 0, PACK)
        quantise_weight("im", 1, 1, 0, 2)
        quantise_weight("im", 1, 1, 2, 2)
        quantise_power(0, 1, 0, BANK)
        for g in range(2):
            cast_filters(g)

        squares_by_half("re", 1, 0, ["raw_im00"], BANK, (0, 1, 2, 3))
        squares_by_half("im", 1, 0, ["late_squares"], WIDE, (0, 1, 2, 3))
        squares_by_half("re", 1, 1, ["raw_im10"], BANK, (4, 5, 6, 7))
        quantise_filters(0)
        add_squares(1, 0, 0, WIDE)
        quantise_filters(1)
        quantise_power(1, 0, 0, WIDE)
        filter_bank(0, WIDE, 2)
        squares_by_half("im", 1, 1, ["raw_re01"], WIDE, (4, 5, 0, 1))
        add_squares(1, 0, WIDE, WIDE)
        add_squares(1, 1, 0, NARROW)
        quantise_power(1, 0, WIDE, WIDE)
        two_bank_filter(WIDE, WIDE, (3, 7))
        for lo, bank in zip(range(0, BANK, NARROW), (6, 2, 4, 0)):
            if lo > 0:
                add_squares(1, 1, lo, NARROW)
            quantise_power(1, 1, lo, NARROW)
            if lo < BANK - 2 * NARROW:
                filter_bank(BANK + lo, NARROW, bank)
            else:
                split_filter_bank(BANK + lo, NARROW, bank)
